import numpy as np
import ml_dtypes


def mxq(x, axis, fmt="e4m3"):
    dtype, down = {"e4m3": (ml_dtypes.float8_e4m3fn, 7), "e5m2": (ml_dtypes.float8_e5m2, 14)}[fmt]
    v = np.moveaxis(np.asarray(x, np.float32).astype(ml_dtypes.bfloat16).astype(np.float64), axis, -1)
    blocks = v.reshape(v.shape[:-1] + (-1, 32))
    amax = np.abs(blocks).max(-1, keepdims=True)
    byte = np.maximum(np.where(amax > 0, np.frexp(amax)[1] - 1 + 127, 0) - down, 1)
    scale = np.exp2(byte - 127.0)
    codes = (blocks / scale).astype(np.float32).astype(dtype).astype(np.float64)
    return np.moveaxis((codes * scale).reshape(v.shape), -1, axis)


WIDE = False


def mx_kscale(k):
    if not WIDE:
        return np.ones(k)
    levels = np.array([10, -10, 5, -5, 0])
    if k % 512:
        return np.exp2(np.random.permutation(np.resize(levels, k // 32))).repeat(32)
    a = np.empty((k // 512, 16))
    for p in range(k // 512):
        a[p, :8] = np.random.permutation(np.resize(levels, 8))
        for g in range(8):
            far = levels[np.abs(levels - a[p, g]) >= 10]
            a[p, g + 8] = far[np.random.randint(len(far))]
    return np.exp2(a.ravel()).repeat(32)


def f64(x):
    return np.asarray(x).astype(np.float64)


def striped(idx):
    return np.tile(idx.reshape(-1, 16).T, (8, 1)).astype(np.uint16)


def unstriped(offs):
    return offs[:16].T.reshape(-1).astype(np.int64)


def pack_weight(w):
    k, n = w.shape
    w = f64(np.asarray(w, np.float32).astype(ml_dtypes.bfloat16)).reshape(k // 32, 32, n)
    amax = np.abs(w).max(1)
    byte = np.clip(np.where(amax > 0, np.frexp(amax)[1] - 1 + 127 - 7, 1), 1, 254)
    scaled = (w * np.exp2(127.0 - byte)[:, None, :]).reshape(k, n).astype(np.float32)
    words = np.ascontiguousarray(scaled.reshape(k // 512, 128, 4, n).transpose(0, 1, 3, 2)).astype(ml_dtypes.float8_e4m3fn).view(np.uint8)
    return words, np.ascontiguousarray(byte.astype(np.uint8).reshape(k // 512, 16, n))


def unpack_weight(words, scales):
    g, p, n, _ = words.shape
    vals = np.ascontiguousarray(words).view(ml_dtypes.float8_e4m3fn).astype(np.float64) * np.repeat(np.exp2(scales.astype(np.float64) - 127.0), 8, axis=1)[..., None]
    return vals.transpose(0, 1, 3, 2).reshape(g * 512, n)


def gelu(v):
    return 0.5 * v * (1.0 + np.tanh(np.sqrt(2.0 / np.pi) * (v + 0.044715 * v**3)))


K, T, S, H, N = 512, 4096, 1024, 1024, 128


def setup_inputs():
    n = np.random.standard_normal
    s = mx_kscale(K)[:, None]
    u = mx_kscale(H)
    packed = pack_weight(n((K, T)) * s)
    return {
        "x_words": packed[0],
        "x_scales": packed[1],
        "w1": (n((K, H)) / np.sqrt(K) / s * u).astype(np.float32),
        "w2": (n((H, N)) / np.sqrt(H) / u[:, None]).astype(np.float32),
        "offs": striped(np.sort(np.random.permutation(T)[:S])),
    }


def reference(x_words, x_scales, w1, w2, offs):
    idx = unstriped(offs)
    xq = unpack_weight(x_words, x_scales)[:, idx]
    h = gelu(mxq(f64(w1), 0, "e4m3").T @ xq)
    y = mxq(f64(w2), 0, "e4m3").T @ mxq(h, 0, "e4m3")
    return y

@@ -1,0 +1,155 @@
+from contextlib import ExitStack
+
+import concourse.mybir as mybir
+
+K, T, S, H, N = 512, 4096, 1024, 1024, 128
+FLOPS = 2 * S * (K * H + H * N)
+
+F32 = mybir.dt.float32
+BF16 = mybir.dt.bfloat16
+I32 = mybir.dt.int32
+U32 = mybir.dt.uint32
+U16 = mybir.dt.uint16
+U8 = mybir.dt.uint8
+FP8X4 = mybir.dt.float8_e4m3fn_x4
+GELU = mybir.ActivationFunctionType.Gelu_apprx_tanh
+
+P = 128
+PACK = 4
+PASS = P * PACK
+TOK = 128
+FIRST = 512
+FIRST_WINDOW = T - S + FIRST
+CHUNKS = (256, 256, 256, 128, 128)
+
+
+def tile_picked_pick_mlp_gelu_srt_p_kernel(tc, x_words, x_scales, w1, w2, offs, out):
+    nc = tc.nc
+    with ExitStack() as ctx:
+        keep = ctx.enter_context(tc.tile_pool(name="keep", bufs=1))
+        hpsum = ctx.enter_context(tc.psum_pool(name="hpsum", bufs=5))
+        ypsum = ctx.enter_context(tc.psum_pool(name="ypsum", bufs=3))
+
+        offsets = keep.tile([P, S // 16], U16, name="offsets")
+        word_table = keep.tile([P, T], I32, name="word_table", align_bytes=64)
+        scale_table = keep.tile([P, T // 4], I32, name="scale_table", tag="scale_then_codes", align_bytes=64)
+        w1_raw = [keep.tile([P, PACK, PASS], F32, name="w1_raw0", tag="w1_raw", align_bytes=64)]
+
+        nc.vector.memset(scale_table[:], 0)
+        warm_in = keep.tile([P, 1], F32, name="warm_in")
+        warm_out = keep.tile([P, 1], F32, name="warm_out")
+        nc.vector.memset(warm_in[:], 0.0)
+
+        words_hbm = x_words[0].rearrange("p c r -> p (c r)").bitcast(I32)
+        scales_hbm = x_scales[0].bitcast(I32)
+        w1_hbm = w1.rearrange("(p j) c -> p j c", j=PACK)
+
+        nc.sync.dma_start(offsets[:], offs)
+        nc.sync.dma_start(w1_raw[0][:], w1_hbm[:, :, 0:PASS])
+        for r in range(4):
+            nc.scalar.dma_start(scale_table[r:P:32, :], scales_hbm[r:16:4, :])
+        nc.scalar.activation(warm_out[:], warm_in[:], GELU)
+        nc.sync.dma_start(word_table[:, 0:FIRST_WINDOW], words_hbm[:, 0:FIRST_WINDOW])
+        nc.sync.dma_start(word_table[:, FIRST_WINDOW:T], words_hbm[:, FIRST_WINDOW:T])
+
+        w1_grouped = [keep.tile([P, PASS * PACK], BF16, name="w1_grouped%d" % g, tag="grouped%d" % g, align_bytes=64) for g in range(2)]
+        w1_codes = [keep.tile([P, PASS], U32, name="w1_codes%d" % g, align_bytes=64) for g in range(2)]
+        w1_scales = [keep.tile([P, PASS], U8, name="w1_scales%d" % g, align_bytes=64) for g in range(2)]
+
+        def group_w1(g):
+            nc.vector.tensor_copy(
+                out=w1_grouped[g][:].rearrange("p (t m j) -> p m t j", t=PACK, j=PACK),
+                in_=w1_raw[g][:].rearrange("p j (m t) -> p m t j", t=PACK),
+            )
+
+        def quantize_w1(g):
+            nc.vector.quantize_mx(out=w1_codes[g][:].bitcast(FP8X4), scales=w1_scales[g][:], in_=w1_grouped[g][:])
+
+        x_planes = keep.tile([P, S], U8, name="x_planes", align_bytes=64)
+
+        group_w1(0)
+        quantize_w1(0)
+        w1_raw.append(keep.tile([P, PACK, PASS], F32, name="w1_raw1", tag="w1_raw", align_bytes=64))
+        w2_raw = keep.tile([P, 2, PACK, N], F32, name="w2_raw", tag="grouped0", align_bytes=64)
+        nc.sync.dma_start(w1_raw[1][:], w1_hbm[:, :, PASS:H])
+        nc.sync.dma_start(w2_raw[:], w2.rearrange("(g p t) n -> p g t n", g=2, t=PACK))
+        nc.vector.tensor_copy(x_planes[:], scale_table[:].bitcast(U8).indirect(offsets[:]))
+        x_codes = keep.tile([P, S], U32, name="x_codes", tag="scale_then_codes", align_bytes=64)
+        nc.vector.tensor_copy(
+            x_codes[:, 0:FIRST], word_table[:, 0:FIRST_WINDOW].bitcast(U32).indirect(offsets[:, 0 : FIRST // 16])
+        )
+        nc.vector.tensor_copy(
+            x_codes[:, FIRST:S], word_table[:].bitcast(U32).indirect(offsets[:, FIRST // 16 : S // 16])
+        )
+
+        starts = [sum(CHUNKS[:c]) for c in range(len(CHUNKS))]
+        h_bf = [[keep.tile([P, w * PACK], BF16, name="h_bf%d_%d" % (g, c), align_bytes=64) for c, w in enumerate(CHUNKS)] for g in range(2)]
+        h_codes = [[keep.tile([P, w], U32, name="h_codes%d_%d" % (g, c), align_bytes=64) for c, w in enumerate(CHUNKS)] for g in range(2)]
+        h_scales = [[keep.tile([P, w], U8, name="h_scales%d_%d" % (g, c), align_bytes=64) for c, w in enumerate(CHUNKS)] for g in range(2)]
+
+        def layer1(g, c):
+            for s in range(CHUNKS[c] // TOK):
+                cols = slice(starts[c] + s * TOK, starts[c] + (s + 1) * TOK)
+                bank = hpsum.tile([P, PACK, TOK], F32, name="hbank")
+                for t in range(PACK):
+                    nc.tensor.matmul_mx(
+                        out=bank[:, t, :],
+                        lhsT=w1_codes[g][:, t * P : (t + 1) * P].bitcast(FP8X4),
+                        lhsT_scale=w1_scales[g][:, t * P : (t + 1) * P],
+                        rhs=x_codes[:, cols].bitcast(FP8X4),
+                        rhs_scale=x_planes[:, cols],
+                        start=True,
+                        stop=True,
+                    )
+                nc.scalar.activation(
+                    h_bf[g][c][:, s * TOK * PACK : (s + 1) * TOK * PACK].rearrange("p (n t) -> p n t", t=PACK),
+                    bank[:].rearrange("p t n -> p n t"),
+                    GELU,
+                )
+
+        def quantize_h(g, c):
+            nc.vector.quantize_mx(out=h_codes[g][c][:].bitcast(FP8X4), scales=h_scales[g][c][:], in_=h_bf[g][c][:])
+
+        for c in range(len(CHUNKS)):
+            layer1(0, c)
+
+        w2_grouped = keep.tile([P, 2 * N * PACK], BF16, name="w2_grouped", align_bytes=64)
+        w2_codes = keep.tile([P, 2 * N], U32, name="w2_codes", align_bytes=64)
+        w2_scales = keep.tile([P, 2 * N], U8, name="w2_scales", align_bytes=64)
+        group_w1(1)
+        quantize_w1(1)
+        nc.vector.tensor_copy(
+            out=w2_grouped[:].rearrange("p (g n t) -> p g n t", g=2, t=PACK),
+            in_=w2_raw[:].rearrange("p g t n -> p g n t"),
+        )
+        quantize_h(0, 0)
+        nc.vector.quantize_mx(out=w2_codes[:].bitcast(FP8X4), scales=w2_scales[:], in_=w2_grouped[:])
+        for c in range(1, len(CHUNKS)):
+            quantize_h(0, c)
+
+        def layer2(c):
+            w = CHUNKS[c]
+            acc = ypsum.tile([P, w], F32, name="ybank")
+            for g in range(2):
+                nc.tensor.matmul_mx(
+                    out=acc[:],
+                    lhsT=w2_codes[:, g * N : (g + 1) * N].bitcast(FP8X4),
+                    lhsT_scale=w2_scales[:, g * N : (g + 1) * N],
+                    rhs=h_codes[g][c][:].bitcast(FP8X4),
+                    rhs_scale=h_scales[g][c][:],
+                    start=(g == 0),
+                    stop=(g == 1),
+                )
+            y = keep.tile([P, w], F32, name="y%d" % c)
+            if c >= len(CHUNKS) - 2:
+                nc.scalar.copy(y[:], acc[:])
+            else:
+                nc.vector.tensor_copy(y[:], acc[:])
+            nc.sync.dma_start(out[:, starts[c] : starts[c] + w], y[:])
+
+        for c in range(len(CHUNKS)):
+            layer1(1, c)
+            quantize_h(1, c)
+            if c >= 1:
+                layer2(c - 1)
+        layer2(len(CHUNKS) - 1)

@@ -18,7 +18,7 @@ P = 128
 PACK = 4
 PASS = P * PACK
 TOK = 128
-FIRST = 512
+FIRST = 448
 FIRST_WINDOW = T - S + FIRST
 CHUNKS = (256, 256, 256, 128, 128)
 
@@ -31,14 +31,15 @@ def tile_picked_pick_mlp_gelu_srt_p_kernel(tc, x_words, x_scales, w1, w2, offs, 
         ypsum = ctx.enter_context(tc.psum_pool(name="ypsum", bufs=3))
 
         offsets = keep.tile([P, S // 16], U16, name="offsets")
-        word_table = keep.tile([P, T], I32, name="word_table", align_bytes=64)
-        scale_table = keep.tile([P, T // 4], I32, name="scale_table", tag="scale_then_codes", align_bytes=64)
+        scale_table = keep.tile([P, T // 4], I32, name="scale_table", tag="chain", align_bytes=64)
         w1_raw = [keep.tile([P, PACK, PASS], F32, name="w1_raw0", tag="w1_raw", align_bytes=64)]
 
         nc.vector.memset(scale_table[:], 0)
         warm_in = keep.tile([P, 1], F32, name="warm_in")
         warm_out = keep.tile([P, 1], F32, name="warm_out")
         nc.vector.memset(warm_in[:], 0.0)
+        x_planes = keep.tile([P, S // 4], I32, name="x_planes", align_bytes=64)
+        nc.vector.memset(x_planes[:], 0)
 
         words_hbm = x_words[0].rearrange("p c r -> p (c r)").bitcast(I32)
         scales_hbm = x_scales[0].bitcast(I32)
@@ -46,35 +47,38 @@ def tile_picked_pick_mlp_gelu_srt_p_kernel(tc, x_words, x_scales, w1, w2, offs, 
 
         nc.sync.dma_start(offsets[:], offs)
         nc.sync.dma_start(w1_raw[0][:], w1_hbm[:, :, 0:PASS])
-        for r in range(4):
-            nc.scalar.dma_start(scale_table[r:P:32, :], scales_hbm[r:16:4, :])
+        nc.scalar.dma_start(scale_table[4:P:8, :], scales_hbm)
         nc.scalar.activation(warm_out[:], warm_in[:], GELU)
+        word_table = keep.tile([P, T], I32, name="word_table", align_bytes=64)
         nc.sync.dma_start(word_table[:, 0:FIRST_WINDOW], words_hbm[:, 0:FIRST_WINDOW])
         nc.sync.dma_start(word_table[:, FIRST_WINDOW:T], words_hbm[:, FIRST_WINDOW:T])
 
-        w1_grouped = [keep.tile([P, PASS * PACK], BF16, name="w1_grouped%d" % g, tag="grouped%d" % g, align_bytes=64) for g in range(2)]
+        w1_grouped = []
         w1_codes = [keep.tile([P, PASS], U32, name="w1_codes%d" % g, align_bytes=64) for g in range(2)]
         w1_scales = [keep.tile([P, PASS], U8, name="w1_scales%d" % g, align_bytes=64) for g in range(2)]
 
-        def group_w1(g):
+        def group_w1(g, tag):
+            w1_grouped.append(keep.tile([P, PASS * PACK], BF16, name="w1_grouped%d" % g, tag=tag, align_bytes=64))
             nc.vector.tensor_copy(
-                out=w1_grouped[g][:].rearrange("p (t m j) -> p m t j", t=PACK, j=PACK),
-                in_=w1_raw[g][:].rearrange("p j (m t) -> p m t j", t=PACK),
+                out=w1_grouped[g][:].rearrange("p (t m j) -> p m j t", t=PACK, j=PACK),
+                in_=w1_raw[g][:].rearrange("p j (m t) -> p m j t", t=PACK),
             )
 
         def quantize_w1(g):
             nc.vector.quantize_mx(out=w1_codes[g][:].bitcast(FP8X4), scales=w1_scales[g][:], in_=w1_grouped[g][:])
 
-        x_planes = keep.tile([P, S], U8, name="x_planes", align_bytes=64)
+        picked_scales = keep.tile([P, S], U8, name="picked_scales", tag="picked_then_w2", align_bytes=64)
 
-        group_w1(0)
+        nc.vector.tensor_copy(picked_scales[:], scale_table[:].bitcast(U8).indirect(offsets[:]))
+        for r in range(4):
+            nc.scalar.dma_start(x_planes[r:P:32, :], picked_scales[:].bitcast(I32)[4 + 8 * r : P : 32, :])
+        group_w1(0, "chain")
         quantize_w1(0)
         w1_raw.append(keep.tile([P, PACK, PASS], F32, name="w1_raw1", tag="w1_raw", align_bytes=64))
-        w2_raw = keep.tile([P, 2, PACK, N], F32, name="w2_raw", tag="grouped0", align_bytes=64)
+        w2_raw = keep.tile([P, 2, PACK, N], F32, name="w2_raw", tag="picked_then_w2", align_bytes=64)
         nc.sync.dma_start(w1_raw[1][:], w1_hbm[:, :, PASS:H])
         nc.sync.dma_start(w2_raw[:], w2.rearrange("(g p t) n -> p g t n", g=2, t=PACK))
-        nc.vector.tensor_copy(x_planes[:], scale_table[:].bitcast(U8).indirect(offsets[:]))
-        x_codes = keep.tile([P, S], U32, name="x_codes", tag="scale_then_codes", align_bytes=64)
+        x_codes = keep.tile([P, S], U32, name="x_codes", tag="chain", align_bytes=64)
         nc.vector.tensor_copy(
             x_codes[:, 0:FIRST], word_table[:, 0:FIRST_WINDOW].bitcast(U32).indirect(offsets[:, 0 : FIRST // 16])
         )
@@ -97,7 +101,7 @@ def tile_picked_pick_mlp_gelu_srt_p_kernel(tc, x_words, x_scales, w1, w2, offs, 
                         lhsT=w1_codes[g][:, t * P : (t + 1) * P].bitcast(FP8X4),
                         lhsT_scale=w1_scales[g][:, t * P : (t + 1) * P],
                         rhs=x_codes[:, cols].bitcast(FP8X4),
-                        rhs_scale=x_planes[:, cols],
+                        rhs_scale=x_planes[:].bitcast(U8)[:, cols],
                         start=True,
                         stop=True,
                     )
@@ -116,7 +120,7 @@ def tile_picked_pick_mlp_gelu_srt_p_kernel(tc, x_words, x_scales, w1, w2, offs, 
         w2_grouped = keep.tile([P, 2 * N * PACK], BF16, name="w2_grouped", align_bytes=64)
         w2_codes = keep.tile([P, 2 * N], U32, name="w2_codes", align_bytes=64)
         w2_scales = keep.tile([P, 2 * N], U8, name="w2_scales", align_bytes=64)
-        group_w1(1)
+        group_w1(1, "grouped1")
         quantize_w1(1)
         nc.vector.tensor_copy(
             out=w2_grouped[:].rearrange("p (g n t) -> p g n t", g=2, t=PACK),

@@ -27,11 +27,12 @@ def tile_picked_pick_mlp_gelu_srt_p_kernel(tc, x_words, x_scales, w1, w2, offs, 
     nc = tc.nc
     with ExitStack() as ctx:
         keep = ctx.enter_context(tc.tile_pool(name="keep", bufs=1))
+        reuse = ctx.enter_context(tc.tile_pool(name="reuse", bufs=1))
         hpsum = ctx.enter_context(tc.psum_pool(name="hpsum", bufs=5))
         ypsum = ctx.enter_context(tc.psum_pool(name="ypsum", bufs=3))
 
         offsets = keep.tile([P, S // 16], U16, name="offsets")
-        scale_table = keep.tile([P, T // 4], I32, name="scale_table", tag="chain", align_bytes=64)
+        scale_table = reuse.tile([P, T // 4], I32, name="scale_table", offset=0, align_bytes=64)
         w1_raw = [keep.tile([P, PACK, PASS], F32, name="w1_raw0", tag="w1_raw", align_bytes=64)]
 
         nc.vector.memset(scale_table[:], 0)
@@ -54,15 +55,20 @@ def tile_picked_pick_mlp_gelu_srt_p_kernel(tc, x_words, x_scales, w1, w2, offs, 
         nc.sync.dma_start(word_table[:, FIRST_WINDOW:T], words_hbm[:, FIRST_WINDOW:T])
 
         w1_grouped = []
-        w1_codes = [keep.tile([P, PASS], U32, name="w1_codes%d" % g, align_bytes=64) for g in range(2)]
+        w1_codes = [
+            reuse.tile([P, PASS], U32, name="w1_codes0", offset=0, align_bytes=64),
+            keep.tile([P, PASS], U32, name="w1_codes1", align_bytes=64),
+        ]
         w1_scales = [keep.tile([P, PASS], U8, name="w1_scales%d" % g, align_bytes=64) for g in range(2)]
 
-        def group_w1(g, tag):
+        def group_w1(g, tag, pieces):
             w1_grouped.append(keep.tile([P, PASS * PACK], BF16, name="w1_grouped%d" % g, tag=tag, align_bytes=64))
-            nc.vector.tensor_copy(
-                out=w1_grouped[g][:].rearrange("p (t m j) -> p m j t", t=PACK, j=PACK),
-                in_=w1_raw[g][:].rearrange("p j (m t) -> p m j t", t=PACK),
-            )
+            for q in range(pieces):
+                ms = slice(q * P // pieces, (q + 1) * P // pieces)
+                nc.vector.tensor_copy(
+                    out=w1_grouped[g][:].rearrange("p (t m j) -> p m j t", t=PACK, j=PACK)[:, ms],
+                    in_=w1_raw[g][:].rearrange("p j (m t) -> p m j t", t=PACK)[:, ms],
+                )
 
         def quantize_w1(g):
             nc.vector.quantize_mx(out=w1_codes[g][:].bitcast(FP8X4), scales=w1_scales[g][:], in_=w1_grouped[g][:])
@@ -72,13 +78,22 @@ def tile_picked_pick_mlp_gelu_srt_p_kernel(tc, x_words, x_scales, w1, w2, offs, 
         nc.vector.tensor_copy(picked_scales[:], scale_table[:].bitcast(U8).indirect(offsets[:]))
         for r in range(4):
             nc.scalar.dma_start(x_planes[r:P:32, :], picked_scales[:].bitcast(I32)[4 + 8 * r : P : 32, :])
-        group_w1(0, "chain")
-        quantize_w1(0)
+        low = reuse.tile([P, 2 * PASS], BF16, name="low", offset=4096, align_bytes=64)
+        high = reuse.tile([P, 2 * PASS], BF16, name="high", offset=2048, align_bytes=64)
+        raw0 = w1_raw[0][:].rearrange("p j (m t) -> p m j t", t=PACK)
+        nc.scalar.copy(low[:].rearrange("p (t m j) -> p m j t", t=2, j=PACK), raw0[:, :, :, 0:2])
+        nc.vector.tensor_copy(out=high[:].rearrange("p (t m j) -> p m j t", t=2, j=PACK), in_=raw0[:, :, :, 2:4])
+        nc.vector.quantize_mx(out=w1_codes[0][:, 0:256].bitcast(FP8X4), scales=w1_scales[0][:, 0:256], in_=low[:])
+        nc.vector.quantize_mx(out=w1_codes[0][:, 256:512].bitcast(FP8X4), scales=w1_scales[0][:, 256:512], in_=high[:])
+        w1_grouped.append(low)
         w1_raw.append(keep.tile([P, PACK, PASS], F32, name="w1_raw1", tag="w1_raw", align_bytes=64))
         w2_raw = keep.tile([P, 2, PACK, N], F32, name="w2_raw", tag="picked_then_w2", align_bytes=64)
-        nc.sync.dma_start(w1_raw[1][:], w1_hbm[:, :, PASS:H])
+        for q in range(2):
+            nc.sync.dma_start(
+                w1_raw[1][:, :, q * 256 : (q + 1) * 256], w1_hbm[:, :, PASS + q * 256 : PASS + (q + 1) * 256]
+            )
         nc.sync.dma_start(w2_raw[:], w2.rearrange("(g p t) n -> p g t n", g=2, t=PACK))
-        x_codes = keep.tile([P, S], U32, name="x_codes", tag="chain", align_bytes=64)
+        x_codes = reuse.tile([P, S], U32, name="x_codes", offset=2048, align_bytes=64)
         nc.vector.tensor_copy(
             x_codes[:, 0:FIRST], word_table[:, 0:FIRST_WINDOW].bitcast(U32).indirect(offsets[:, 0 : FIRST // 16])
         )
@@ -109,6 +124,7 @@ def tile_picked_pick_mlp_gelu_srt_p_kernel(tc, x_words, x_scales, w1, w2, offs, 
                     h_bf[g][c][:, s * TOK * PACK : (s + 1) * TOK * PACK].rearrange("p (n t) -> p n t", t=PACK),
                     bank[:].rearrange("p t n -> p n t"),
                     GELU,
+                    bias=warm_out[:],
                 )
 
         def quantize_h(g, c):
@@ -117,11 +133,11 @@ def tile_picked_pick_mlp_gelu_srt_p_kernel(tc, x_words, x_scales, w1, w2, offs, 
         for c in range(len(CHUNKS)):
             layer1(0, c)
 
-        w2_grouped = keep.tile([P, 2 * N * PACK], BF16, name="w2_grouped", align_bytes=64)
         w2_codes = keep.tile([P, 2 * N], U32, name="w2_codes", align_bytes=64)
         w2_scales = keep.tile([P, 2 * N], U8, name="w2_scales", align_bytes=64)
-        group_w1(1, "grouped1")
+        group_w1(1, "grouped1", 2)
         quantize_w1(1)
+        w2_grouped = keep.tile([P, 2 * N * PACK], BF16, name="w2_grouped", tag="grouped1", align_bytes=64)
         nc.vector.tensor_copy(
             out=w2_grouped[:].rearrange("p (g n t) -> p g n t", g=2, t=PACK),
             in_=w2_raw[:].rearrange("p g t n -> p g n t"),

@@ -35,7 +35,7 @@ def tile_picked_pick_mlp_gelu_srt_p_kernel(tc, x_words, x_scales, w1, w2, offs, 
         scale_table = reuse.tile([P, T // 4], I32, name="scale_table", offset=0, align_bytes=64)
         w1_raw = [keep.tile([P, PACK, PASS], F32, name="w1_raw0", tag="w1_raw", align_bytes=64)]
 
-        nc.vector.memset(scale_table[:], 0)
+        nc.vector.memset(scale_table[0:112, :], 0)
         warm_in = keep.tile([P, 1], F32, name="warm_in")
         warm_out = keep.tile([P, 1], F32, name="warm_out")
         nc.vector.memset(warm_in[:], 0.0)
@@ -48,7 +48,7 @@ def tile_picked_pick_mlp_gelu_srt_p_kernel(tc, x_words, x_scales, w1, w2, offs, 
 
         nc.sync.dma_start(offsets[:], offs)
         nc.sync.dma_start(w1_raw[0][:], w1_hbm[:, :, 0:PASS])
-        nc.scalar.dma_start(scale_table[4:P:8, :], scales_hbm)
+        nc.scalar.dma_start(scale_table[112:P, :], scales_hbm)
         nc.scalar.activation(warm_out[:], warm_in[:], GELU)
         word_table = keep.tile([P, T], I32, name="word_table", align_bytes=64)
         nc.sync.dma_start(word_table[:, 0:FIRST_WINDOW], words_hbm[:, 0:FIRST_WINDOW])
@@ -77,7 +77,7 @@ def tile_picked_pick_mlp_gelu_srt_p_kernel(tc, x_words, x_scales, w1, w2, offs, 
 
         nc.vector.tensor_copy(picked_scales[:], scale_table[:].bitcast(U8).indirect(offsets[:]))
         for r in range(4):
-            nc.scalar.dma_start(x_planes[r:P:32, :], picked_scales[:].bitcast(I32)[4 + 8 * r : P : 32, :])
+            nc.scalar.dma_start(x_planes[r:P:32, :], picked_scales[:].bitcast(I32)[112 + r : P : 4, :])
         low = reuse.tile([P, 2 * PASS], BF16, name="low", offset=4096, align_bytes=64)
         high = reuse.tile([P, 2 * PASS], BF16, name="high", offset=2048, align_bytes=64)
         raw0 = w1_raw[0][:].rearrange("p j (m t) -> p m j t", t=PACK)

@@ -77,7 +77,7 @@ def tile_picked_pick_mlp_gelu_srt_p_kernel(tc, x_words, x_scales, w1, w2, offs, 
 
         nc.vector.tensor_copy(picked_scales[:], scale_table[:].bitcast(U8).indirect(offsets[:]))
         for r in range(4):
-            nc.scalar.dma_start(x_planes[r:P:32, :], picked_scales[:].bitcast(I32)[112 + r : P : 4, :])
+            nc.sync.dma_start(x_planes[r:P:32, :], picked_scales[:].bitcast(I32)[112 + r : P : 4, :])
         low = reuse.tile([P, 2 * PASS], BF16, name="low", offset=4096, align_bytes=64)
         high = reuse.tile([P, 2 * PASS], BF16, name="high", offset=2048, align_bytes=64)
         raw0 = w1_raw[0][:].rearrange("p j (m t) -> p m j t", t=PACK)

@@ -124,7 +124,7 @@ def tile_picked_pick_mlp_gelu_srt_p_kernel(tc, x_words, x_scales, w1, w2, offs, 
                     h_bf[g][c][:, s * TOK * PACK : (s + 1) * TOK * PACK].rearrange("p (n t) -> p n t", t=PACK),
                     bank[:].rearrange("p t n -> p n t"),
                     GELU,
-                    bias=warm_out[:],
+                    bias=warm_out[:] if (g, c, s) == (0, 0, 0) else 0.0,
                 )
 
         def quantize_h(g, c):

@@ -61,8 +61,8 @@ def tile_picked_pick_mlp_gelu_srt_p_kernel(tc, x_words, x_scales, w1, w2, offs, 
         ]
         w1_scales = [keep.tile([P, PASS], U8, name="w1_scales%d" % g, align_bytes=64) for g in range(2)]
 
-        def group_w1(g, tag, pieces):
-            w1_grouped.append(keep.tile([P, PASS * PACK], BF16, name="w1_grouped%d" % g, tag=tag, align_bytes=64))
+        def group_w1(g, pieces):
+            w1_grouped.append(reuse.tile([P, PASS * PACK], BF16, name="w1_grouped%d" % g, offset=6144, align_bytes=64))
             for q in range(pieces):
                 ms = slice(q * P // pieces, (q + 1) * P // pieces)
                 nc.vector.tensor_copy(
@@ -104,7 +104,10 @@ def tile_picked_pick_mlp_gelu_srt_p_kernel(tc, x_words, x_scales, w1, w2, offs, 
         starts = [sum(CHUNKS[:c]) for c in range(len(CHUNKS))]
         h_bf = [[keep.tile([P, w * PACK], BF16, name="h_bf%d_%d" % (g, c), align_bytes=64) for c, w in enumerate(CHUNKS)] for g in range(2)]
         h_codes = [[keep.tile([P, w], U32, name="h_codes%d_%d" % (g, c), align_bytes=64) for c, w in enumerate(CHUNKS)] for g in range(2)]
-        h_scales = [[keep.tile([P, w], U8, name="h_scales%d_%d" % (g, c), align_bytes=64) for c, w in enumerate(CHUNKS)] for g in range(2)]
+        h_scales = [
+            [reuse.tile([P, w], U8, name="h_scales0_%d" % c, offset=8192 + starts[c], align_bytes=64) for c, w in enumerate(CHUNKS)],
+            [keep.tile([P, w], U8, name="h_scales1_%d" % c, align_bytes=64) for c, w in enumerate(CHUNKS)],
+        ]
 
         def layer1(g, c):
             for s in range(CHUNKS[c] // TOK):
@@ -135,9 +138,9 @@ def tile_picked_pick_mlp_gelu_srt_p_kernel(tc, x_words, x_scales, w1, w2, offs, 
 
         w2_codes = keep.tile([P, 2 * N], U32, name="w2_codes", align_bytes=64)
         w2_scales = keep.tile([P, 2 * N], U8, name="w2_scales", align_bytes=64)
-        group_w1(1, "grouped1", 2)
+        group_w1(1, 2)
         quantize_w1(1)
-        w2_grouped = keep.tile([P, 2 * N * PACK], BF16, name="w2_grouped", tag="grouped1", align_bytes=64)
+        w2_grouped = reuse.tile([P, 2 * N * PACK], BF16, name="w2_grouped", offset=6144, align_bytes=64)
         nc.vector.tensor_copy(
             out=w2_grouped[:].rearrange("p (g n t) -> p g n t", g=2, t=PACK),
             in_=w2_raw[:].rearrange("p g t n -> p g n t"),
@@ -150,18 +153,19 @@ def tile_picked_pick_mlp_gelu_srt_p_kernel(tc, x_words, x_scales, w1, w2, offs, 
         def layer2(c):
             w = CHUNKS[c]
             acc = ypsum.tile([P, w], F32, name="ybank")
-            for g in range(2):
+            passes = (0, 1) if c == len(CHUNKS) - 1 else (1, 0)
+            for g in passes:
                 nc.tensor.matmul_mx(
                     out=acc[:],
                     lhsT=w2_codes[:, g * N : (g + 1) * N].bitcast(FP8X4),
                     lhsT_scale=w2_scales[:, g * N : (g + 1) * N],
                     rhs=h_codes[g][c][:].bitcast(FP8X4),
                     rhs_scale=h_scales[g][c][:],
-                    start=(g == 0),
-                    stop=(g == 1),
+                    start=(g == passes[0]),
+                    stop=(g == passes[1]),
                 )
             y = keep.tile([P, w], F32, name="y%d" % c)
-            if c >= len(CHUNKS) - 2:
+            if c >= len(CHUNKS) - 3:
                 nc.scalar.copy(y[:], acc[:])
             else:
                 nc.vector.tensor_copy(y[:], acc[:])

@@ -61,17 +61,22 @@ def tile_picked_pick_mlp_gelu_srt_p_kernel(tc, x_words, x_scales, w1, w2, offs, 
         ]
         w1_scales = [keep.tile([P, PASS], U8, name="w1_scales%d" % g, align_bytes=64) for g in range(2)]
 
-        def group_w1(g, pieces):
+        def group_and_quantize_w1(g, pieces):
             w1_grouped.append(reuse.tile([P, PASS * PACK], BF16, name="w1_grouped%d" % g, offset=6144, align_bytes=64))
             for q in range(pieces):
                 ms = slice(q * P // pieces, (q + 1) * P // pieces)
-                nc.vector.tensor_copy(
-                    out=w1_grouped[g][:].rearrange("p (t m j) -> p m j t", t=PACK, j=PACK)[:, ms],
-                    in_=w1_raw[g][:].rearrange("p j (m t) -> p m j t", t=PACK)[:, ms],
+                for u in range(2):
+                    nc.vector.tensor_copy(
+                        out=w1_grouped[g][:].rearrange("p (t m j) -> p m j t", t=PACK, j=PACK)[:, ms, :, 2 * u : 2 * u + 2],
+                        in_=w1_raw[g][:].rearrange("p j (m t) -> p m j t", t=PACK)[:, ms, :, 2 * u : 2 * u + 2],
+                    )
+            for u in range(2):
+                cols = slice(u * 2 * P, (u + 1) * 2 * P)
+                nc.vector.quantize_mx(
+                    out=w1_codes[g][:, cols].bitcast(FP8X4),
+                    scales=w1_scales[g][:, cols],
+                    in_=w1_grouped[g][:, u * 2 * P * PACK : (u + 1) * 2 * P * PACK],
                 )
-
-        def quantize_w1(g):
-            nc.vector.quantize_mx(out=w1_codes[g][:].bitcast(FP8X4), scales=w1_scales[g][:], in_=w1_grouped[g][:])
 
         picked_scales = keep.tile([P, S], U8, name="picked_scales", tag="picked_then_w2", align_bytes=64)
 
@@ -102,18 +107,36 @@ def tile_picked_pick_mlp_gelu_srt_p_kernel(tc, x_words, x_scales, w1, w2, offs, 
         )
 
         starts = [sum(CHUNKS[:c]) for c in range(len(CHUNKS))]
-        h_bf = [[keep.tile([P, w * PACK], BF16, name="h_bf%d_%d" % (g, c), align_bytes=64) for c, w in enumerate(CHUNKS)] for g in range(2)]
-        h_codes = [[keep.tile([P, w], U32, name="h_codes%d_%d" % (g, c), align_bytes=64) for c, w in enumerate(CHUNKS)] for g in range(2)]
-        h_scales = [
-            [reuse.tile([P, w], U8, name="h_scales0_%d" % c, offset=8192 + starts[c], align_bytes=64) for c, w in enumerate(CHUNKS)],
-            [keep.tile([P, w], U8, name="h_scales1_%d" % c, align_bytes=64) for c, w in enumerate(CHUNKS)],
+        early_bf = keep.tile([P, S * PACK], BF16, name="early_bf", align_bytes=64)
+        early_codes = keep.tile([P, S], U32, name="early_codes", align_bytes=64)
+        early_scales = reuse.tile([P, S], U8, name="early_scales", offset=8192, align_bytes=64)
+        h_bf = [
+            [early_bf[:, a * PACK : (a + w) * PACK] for a, w in zip(starts, CHUNKS)],
+            [keep.tile([P, w * PACK], BF16, name="h_bf%d" % c, tag="late%d" % c, align_bytes=64) for c, w in enumerate(CHUNKS)],
         ]
+        h_codes = [
+            [early_codes[:, a : a + w] for a, w in zip(starts, CHUNKS)],
+            [keep.tile([P, w], U32, name="h_codes%d" % c, align_bytes=64) for c, w in enumerate(CHUNKS)],
+        ]
+        h_scales = [
+            [early_scales[:, a : a + w] for a, w in zip(starts, CHUNKS)],
+            [keep.tile([P, w], U8, name="h_scales%d" % c, align_bytes=64) for c, w in enumerate(CHUNKS)],
+        ]
+
+        def quantize_early(half):
+            cols = slice(half * S // 2, (half + 1) * S // 2)
+            nc.vector.quantize_mx(
+                out=early_codes[:, cols].bitcast(FP8X4),
+                scales=early_scales[:, cols],
+                in_=early_bf[:, half * S // 2 * PACK : (half + 1) * S // 2 * PACK],
+            )
 
         def layer1(g, c):
             for s in range(CHUNKS[c] // TOK):
                 cols = slice(starts[c] + s * TOK, starts[c] + (s + 1) * TOK)
                 bank = hpsum.tile([P, PACK, TOK], F32, name="hbank")
-                for t in range(PACK):
+                first_of_half = (c, s) == (0, 0)
+                for t in range(PACK) if first_of_half else reversed(range(PACK)):
                     nc.tensor.matmul_mx(
                         out=bank[:, t, :],
                         lhsT=w1_codes[g][:, t * P : (t + 1) * P].bitcast(FP8X4),
@@ -138,17 +161,15 @@ def tile_picked_pick_mlp_gelu_srt_p_kernel(tc, x_words, x_scales, w1, w2, offs, 
 
         w2_codes = keep.tile([P, 2 * N], U32, name="w2_codes", align_bytes=64)
         w2_scales = keep.tile([P, 2 * N], U8, name="w2_scales", align_bytes=64)
-        group_w1(1, 2)
-        quantize_w1(1)
+        group_and_quantize_w1(1, 2)
         w2_grouped = reuse.tile([P, 2 * N * PACK], BF16, name="w2_grouped", offset=6144, align_bytes=64)
         nc.vector.tensor_copy(
-            out=w2_grouped[:].rearrange("p (g n t) -> p g n t", g=2, t=PACK),
-            in_=w2_raw[:].rearrange("p g t n -> p g n t"),
+            out=w2_grouped[:].rearrange("p (g c i t) -> p g c t i", g=2, i=4, t=PACK),
+            in_=w2_raw[:].rearrange("p g t (c i) -> p g c t i", i=4),
         )
-        quantize_h(0, 0)
+        quantize_early(0)
         nc.vector.quantize_mx(out=w2_codes[:].bitcast(FP8X4), scales=w2_scales[:], in_=w2_grouped[:])
-        for c in range(1, len(CHUNKS)):
-            quantize_h(0, c)
+        quantize_early(1)
 
         def layer2(c):
             w = CHUNKS[c]
@@ -164,10 +185,11 @@ def tile_picked_pick_mlp_gelu_srt_p_kernel(tc, x_words, x_scales, w1, w2, offs, 
                     start=(g == passes[0]),
                     stop=(g == passes[1]),
                 )
-            y = keep.tile([P, w], F32, name="y%d" % c)
             if c >= len(CHUNKS) - 3:
+                y = keep.tile([P, w], F32, name="y%d" % c)
                 nc.scalar.copy(y[:], acc[:])
             else:
+                y = keep.tile([P, w], F32, name="y%d" % c, tag="late%d" % (c + 1), align_bytes=64)
                 nc.vector.tensor_copy(y[:], acc[:])
             nc.sync.dma_start(out[:, starts[c] : starts[c] + w], y[:])
 

@@ -91,6 +91,17 @@ def tile_picked_pick_mlp_gelu_srt_p_kernel(tc, x_words, x_scales, w1, w2, offs, 
         nc.vector.quantize_mx(out=w1_codes[0][:, 0:256].bitcast(FP8X4), scales=w1_scales[0][:, 0:256], in_=low[:])
         nc.vector.quantize_mx(out=w1_codes[0][:, 256:512].bitcast(FP8X4), scales=w1_scales[0][:, 256:512], in_=high[:])
         w1_grouped.append(low)
+        warm_bank = ypsum.tile([P, 2 * P], F32, name="ybank")
+        for rep in range(8):
+            nc.tensor.matmul_mx(
+                out=warm_bank[:],
+                lhsT=w1_codes[0][:, 0:P].bitcast(FP8X4),
+                lhsT_scale=w1_scales[0][:, 0:P],
+                rhs=w1_codes[0][:, 2 * P : PASS].bitcast(FP8X4),
+                rhs_scale=w1_scales[0][:, 2 * P : PASS],
+                start=True,
+                stop=True,
+            )
         w1_raw.append(keep.tile([P, PACK, PASS], F32, name="w1_raw1", tag="w1_raw", align_bytes=64))
         w2_raw = keep.tile([P, 2, PACK, N], F32, name="w2_raw", tag="picked_then_w2", align_bytes=64)
         for q in range(2):

@@ -15,12 +15,16 @@ FP8X4 = mybir.dt.float8_e4m3fn_x4
 GELU = mybir.ActivationFunctionType.Gelu_apprx_tanh
 
 P = 128
+HALF = 64
 PACK = 4
 PASS = P * PACK
+QUARTER = 256
 TOK = 128
-FIRST = 448
+FIRST = 512
 FIRST_WINDOW = T - S + FIRST
-CHUNKS = (256, 256, 256, 128, 128)
+SLOT = 3 * HALF
+CHUNKS = ((512, 256), (768, 256), (0, 256), (256, 128), (384, 128))
+WARM = 4
 
 
 def tile_picked_pick_mlp_gelu_srt_p_kernel(tc, x_words, x_scales, w1, w2, offs, out):
@@ -32,8 +36,12 @@ def tile_picked_pick_mlp_gelu_srt_p_kernel(tc, x_words, x_scales, w1, w2, offs, 
         ypsum = ctx.enter_context(tc.psum_pool(name="ypsum", bufs=3))
 
         offsets = keep.tile([P, S // 16], U16, name="offsets")
-        scale_table = reuse.tile([P, T // 4], I32, name="scale_table", offset=0, align_bytes=64)
-        w1_raw = [keep.tile([P, PACK, PASS], F32, name="w1_raw0", tag="w1_raw", align_bytes=64)]
+        scale_table = reuse.tile([P, T // 4], I32, name="scale_table", offset=4096, align_bytes=64)
+        word_table = reuse.tile([P, T], I32, name="word_table", offset=20480, align_bytes=64)
+        quarter_raw = [
+            keep.tile([P, PACK, QUARTER], F32, name="quarter_raw0", align_bytes=64),
+            reuse.tile([P, PACK, QUARTER], F32, name="quarter_raw1", offset=512, align_bytes=64),
+        ]
 
         nc.vector.memset(scale_table[0:112, :], 0)
         warm_in = keep.tile([P, 1], F32, name="warm_in")
@@ -41,98 +49,149 @@ def tile_picked_pick_mlp_gelu_srt_p_kernel(tc, x_words, x_scales, w1, w2, offs, 
         nc.vector.memset(warm_in[:], 0.0)
         x_planes = keep.tile([P, S // 4], I32, name="x_planes", align_bytes=64)
         nc.vector.memset(x_planes[:], 0)
+        early_w_codes = keep.tile([P, PACK * SLOT], U32, name="early_w_codes", align_bytes=64)
+        early_w_scales = keep.tile([P, PACK * SLOT], U8, name="early_w_scales", align_bytes=64)
+        nc.vector.memset(early_w_codes[:].bitcast(I32), 0)
+        nc.vector.memset(early_w_scales[:].bitcast(I32), 0)
+        w2_scales = keep.tile([P, 2 * N], U8, name="w2_scales", align_bytes=64)
+        nc.vector.memset(w2_scales[:].bitcast(I32), 0)
 
         words_hbm = x_words[0].rearrange("p c r -> p (c r)").bitcast(I32)
         scales_hbm = x_scales[0].bitcast(I32)
         w1_hbm = w1.rearrange("(p j) c -> p j c", j=PACK)
 
         nc.sync.dma_start(offsets[:], offs)
-        nc.sync.dma_start(w1_raw[0][:], w1_hbm[:, :, 0:PASS])
+        nc.sync.dma_start(quarter_raw[0][:], w1_hbm[:, :, 0:QUARTER])
         nc.scalar.dma_start(scale_table[112:P, :], scales_hbm)
         nc.scalar.activation(warm_out[:], warm_in[:], GELU)
-        word_table = keep.tile([P, T], I32, name="word_table", align_bytes=64)
         nc.sync.dma_start(word_table[:, 0:FIRST_WINDOW], words_hbm[:, 0:FIRST_WINDOW])
-        nc.sync.dma_start(word_table[:, FIRST_WINDOW:T], words_hbm[:, FIRST_WINDOW:T])
 
-        w1_grouped = []
-        w1_codes = [
-            reuse.tile([P, PASS], U32, name="w1_codes0", offset=0, align_bytes=64),
-            keep.tile([P, PASS], U32, name="w1_codes1", align_bytes=64),
-        ]
-        w1_scales = [keep.tile([P, PASS], U8, name="w1_scales%d" % g, align_bytes=64) for g in range(2)]
-
-        def group_and_quantize_w1(g, pieces):
-            w1_grouped.append(reuse.tile([P, PASS * PACK], BF16, name="w1_grouped%d" % g, offset=6144, align_bytes=64))
-            for q in range(pieces):
-                ms = slice(q * P // pieces, (q + 1) * P // pieces)
-                for u in range(2):
-                    nc.vector.tensor_copy(
-                        out=w1_grouped[g][:].rearrange("p (t m j) -> p m j t", t=PACK, j=PACK)[:, ms, :, 2 * u : 2 * u + 2],
-                        in_=w1_raw[g][:].rearrange("p j (m t) -> p m j t", t=PACK)[:, ms, :, 2 * u : 2 * u + 2],
-                    )
-            for u in range(2):
-                cols = slice(u * 2 * P, (u + 1) * 2 * P)
-                nc.vector.quantize_mx(
-                    out=w1_codes[g][:, cols].bitcast(FP8X4),
-                    scales=w1_scales[g][:, cols],
-                    in_=w1_grouped[g][:, u * 2 * P * PACK : (u + 1) * 2 * P * PACK],
-                )
-
-        picked_scales = keep.tile([P, S], U8, name="picked_scales", tag="picked_then_w2", align_bytes=64)
-
+        picked_scales = reuse.tile([P, S], U8, name="picked_scales", offset=40960, align_bytes=64)
         nc.vector.tensor_copy(picked_scales[:], scale_table[:].bitcast(U8).indirect(offsets[:]))
         for r in range(4):
             nc.sync.dma_start(x_planes[r:P:32, :], picked_scales[:].bitcast(I32)[112 + r : P : 4, :])
-        low = reuse.tile([P, 2 * PASS], BF16, name="low", offset=4096, align_bytes=64)
-        high = reuse.tile([P, 2 * PASS], BF16, name="high", offset=2048, align_bytes=64)
-        raw0 = w1_raw[0][:].rearrange("p j (m t) -> p m j t", t=PACK)
-        nc.scalar.copy(low[:].rearrange("p (t m j) -> p m j t", t=2, j=PACK), raw0[:, :, :, 0:2])
-        nc.vector.tensor_copy(out=high[:].rearrange("p (t m j) -> p m j t", t=2, j=PACK), in_=raw0[:, :, :, 2:4])
-        nc.vector.quantize_mx(out=w1_codes[0][:, 0:256].bitcast(FP8X4), scales=w1_scales[0][:, 0:256], in_=low[:])
-        nc.vector.quantize_mx(out=w1_codes[0][:, 256:512].bitcast(FP8X4), scales=w1_scales[0][:, 256:512], in_=high[:])
-        w1_grouped.append(low)
-        warm_bank = ypsum.tile([P, 2 * P], F32, name="ybank")
-        for rep in range(8):
+        nc.sync.dma_start(quarter_raw[1][:], w1_hbm[:, :, QUARTER:PASS])
+        nc.sync.dma_start(word_table[:, FIRST_WINDOW:T], words_hbm[:, FIRST_WINDOW:T])
+
+        def group_and_quantize_quarter(q, offset):
+            grouped = reuse.tile([P, QUARTER * PACK], BF16, name="quarter_grouped%d" % q, offset=offset, align_bytes=64)
+            for u in range(2):
+                nc.vector.tensor_copy(
+                    out=grouped[:].rearrange("p (t m j) -> p m j t", t=PACK, j=PACK)[:, :, :, 2 * u : 2 * u + 2],
+                    in_=quarter_raw[q][:].rearrange("p j (m t) -> p m j t", t=PACK)[:, :, :, 2 * u : 2 * u + 2],
+                )
+            for t in range(PACK):
+                cols = slice(t * SLOT + (q + 1) * HALF, t * SLOT + (q + 2) * HALF)
+                nc.vector.quantize_mx(
+                    out=early_w_codes[:, cols].bitcast(FP8X4),
+                    scales=early_w_scales[:, cols],
+                    in_=grouped[:, t * HALF * PACK : (t + 1) * HALF * PACK],
+                )
+
+        group_and_quantize_quarter(0, 4608)
+        warm_bank = ypsum.tile([P, PASS], F32, name="ybank")
+        for rep in range(WARM):
             nc.tensor.matmul_mx(
-                out=warm_bank[:],
-                lhsT=w1_codes[0][:, 0:P].bitcast(FP8X4),
-                lhsT_scale=w1_scales[0][:, 0:P],
-                rhs=w1_codes[0][:, 2 * P : PASS].bitcast(FP8X4),
-                rhs_scale=w1_scales[0][:, 2 * P : PASS],
+                out=warm_bank[0:32, :],
+                lhsT=early_w_codes[:, HALF : HALF + 32].bitcast(FP8X4),
+                lhsT_scale=early_w_scales[:, HALF : HALF + 32],
+                rhs=early_w_codes[:, QUARTER : QUARTER + PASS].bitcast(FP8X4),
+                rhs_scale=early_w_scales[:, QUARTER : QUARTER + PASS],
                 start=True,
                 stop=True,
             )
-        w1_raw.append(keep.tile([P, PACK, PASS], F32, name="w1_raw1", tag="w1_raw", align_bytes=64))
-        w2_raw = keep.tile([P, 2, PACK, N], F32, name="w2_raw", tag="picked_then_w2", align_bytes=64)
+        masked_codes = reuse.tile([P, 4 * N], U32, name="masked_codes", offset=4608, align_bytes=64)
+        nc.vector.memset(masked_codes[:].bitcast(I32), 0)
+
+        late_raw = reuse.tile([P, PACK, PASS], F32, name="late_raw", offset=7680, align_bytes=64)
+        w2_raw = reuse.tile([P, 2, PACK, N], F32, name="w2_raw", offset=41472, align_bytes=64)
         for q in range(2):
             nc.sync.dma_start(
-                w1_raw[1][:, :, q * 256 : (q + 1) * 256], w1_hbm[:, :, PASS + q * 256 : PASS + (q + 1) * 256]
+                late_raw[:, :, q * QUARTER : (q + 1) * QUARTER],
+                w1_hbm[:, :, PASS + q * QUARTER : PASS + (q + 1) * QUARTER],
             )
         nc.sync.dma_start(w2_raw[:], w2.rearrange("(g p t) n -> p g t n", g=2, t=PACK))
-        x_codes = reuse.tile([P, S], U32, name="x_codes", offset=2048, align_bytes=64)
-        nc.vector.tensor_copy(
-            x_codes[:, 0:FIRST], word_table[:, 0:FIRST_WINDOW].bitcast(U32).indirect(offsets[:, 0 : FIRST // 16])
-        )
-        nc.vector.tensor_copy(
-            x_codes[:, FIRST:S], word_table[:].bitcast(U32).indirect(offsets[:, FIRST // 16 : S // 16])
-        )
 
-        starts = [sum(CHUNKS[:c]) for c in range(len(CHUNKS))]
+        x_first = keep.tile([P, FIRST], U32, name="x_first", align_bytes=64)
+        nc.vector.tensor_copy(
+            x_first[:], word_table[:, 0:FIRST_WINDOW].bitcast(U32).indirect(offsets[:, 0 : FIRST // 16])
+        )
+        group_and_quantize_quarter(1, 16384)
+        x_rest = reuse.tile([P, S - FIRST], U32, name="x_rest", offset=16384, align_bytes=64)
+        nc.vector.tensor_copy(x_rest[:], word_table[:].bitcast(U32).indirect(offsets[:, FIRST // 16 : S // 16]))
+
+        def tokens(a):
+            codes = x_first[:, a : a + TOK] if a < FIRST else x_rest[:, a - FIRST : a - FIRST + TOK]
+            return codes.bitcast(FP8X4), x_planes[:].bitcast(U8)[:, a : a + TOK]
+
+        def hidden_pass(dst, codes, scales, cols, a):
+            rhs, rhs_scale = tokens(a)
+            nc.tensor.matmul_mx(
+                out=dst,
+                lhsT=codes[:, cols].bitcast(FP8X4),
+                lhsT_scale=scales[:, cols],
+                rhs=rhs,
+                rhs_scale=rhs_scale,
+                start=True,
+                stop=True,
+            )
+
+        def gelu(dst, bank, first=False):
+            nc.scalar.activation(
+                dst.rearrange("p (n t) -> p n t", t=PACK),
+                bank[:].rearrange("p t n -> p n t"),
+                GELU,
+                bias=warm_out[:] if first else 0.0,
+            )
+
         early_bf = keep.tile([P, S * PACK], BF16, name="early_bf", align_bytes=64)
         early_codes = keep.tile([P, S], U32, name="early_codes", align_bytes=64)
-        early_scales = reuse.tile([P, S], U8, name="early_scales", offset=8192, align_bytes=64)
-        h_bf = [
-            [early_bf[:, a * PACK : (a + w) * PACK] for a, w in zip(starts, CHUNKS)],
-            [keep.tile([P, w * PACK], BF16, name="h_bf%d" % c, tag="late%d" % c, align_bytes=64) for c, w in enumerate(CHUNKS)],
-        ]
-        h_codes = [
-            [early_codes[:, a : a + w] for a, w in zip(starts, CHUNKS)],
-            [keep.tile([P, w], U32, name="h_codes%d" % c, align_bytes=64) for c, w in enumerate(CHUNKS)],
-        ]
-        h_scales = [
-            [early_scales[:, a : a + w] for a, w in zip(starts, CHUNKS)],
-            [keep.tile([P, w], U8, name="h_scales%d" % c, align_bytes=64) for c, w in enumerate(CHUNKS)],
-        ]
+        early_scales = reuse.tile([P, S], U8, name="early_scales", offset=22528, align_bytes=64)
+
+        for q in range(2):
+            for s in range(2):
+                upper, lower = (s * TOK, QUARTER + s * TOK) if q == 0 else (QUARTER + s * TOK, s * TOK)
+                bank = hpsum.tile([P, PACK, TOK], F32, name="hbank")
+                order = range(PACK) if s == 0 else range(PACK - 1, -1, -1)
+                for t in order:
+                    a = t * SLOT + q * HALF
+                    hidden_pass(bank[:, t, :], early_w_codes, early_w_scales, slice(a, a + P), lower)
+                for t in order:
+                    a = t * SLOT + (q + 1) * HALF
+                    hidden_pass(bank[0:HALF, t, :], early_w_codes, early_w_scales, slice(a, a + HALF), upper)
+                at = (q * QUARTER + s * TOK) * PACK
+                gelu(early_bf[:, at : at + TOK * PACK], bank, first=(q, s) == (0, 0))
+        for a in range(FIRST, S, TOK):
+            bank = hpsum.tile([P, PACK, TOK], F32, name="hbank")
+            for t in range(PACK):
+                c0 = t * SLOT + HALF
+                hidden_pass(bank[:, t, :], early_w_codes, early_w_scales, slice(c0, c0 + P), a)
+            gelu(early_bf[:, a * PACK : (a + TOK) * PACK], bank)
+
+        late_w_codes = keep.tile([P, PASS], U32, name="late_w_codes", align_bytes=64)
+        late_w_scales = keep.tile([P, PASS], U8, name="late_w_scales", align_bytes=64)
+        late_grouped = reuse.tile([P, PASS * PACK], BF16, name="late_grouped", offset=20480, align_bytes=64)
+        for q in range(2):
+            ms = slice(q * HALF, (q + 1) * HALF)
+            for u in range(2):
+                nc.vector.tensor_copy(
+                    out=late_grouped[:].rearrange("p (t m j) -> p m j t", t=PACK, j=PACK)[:, ms, :, 2 * u : 2 * u + 2],
+                    in_=late_raw[:].rearrange("p j (m t) -> p m j t", t=PACK)[:, ms, :, 2 * u : 2 * u + 2],
+                )
+        for u in range(2):
+            cols = slice(u * 2 * P, (u + 1) * 2 * P)
+            nc.vector.quantize_mx(
+                out=late_w_codes[:, cols].bitcast(FP8X4),
+                scales=late_w_scales[:, cols],
+                in_=late_grouped[:, u * 2 * P * PACK : (u + 1) * 2 * P * PACK],
+            )
+
+        w2_codes = keep.tile([P, 2 * N], U32, name="w2_codes", align_bytes=64)
+        w2_grouped = reuse.tile([P, 2 * N * PACK], BF16, name="w2_grouped", offset=20480, align_bytes=64)
+        nc.vector.tensor_copy(
+            out=w2_grouped[:].rearrange("p (g c i t) -> p g c t i", g=2, i=4, t=PACK),
+            in_=w2_raw[:].rearrange("p g t (c i) -> p g c t i", i=4),
+        )
 
         def quantize_early(half):
             cols = slice(half * S // 2, (half + 1) * S // 2)
@@ -142,59 +201,58 @@ def tile_picked_pick_mlp_gelu_srt_p_kernel(tc, x_words, x_scales, w1, w2, offs, 
                 in_=early_bf[:, half * S // 2 * PACK : (half + 1) * S // 2 * PACK],
             )
 
-        def layer1(g, c):
-            for s in range(CHUNKS[c] // TOK):
-                cols = slice(starts[c] + s * TOK, starts[c] + (s + 1) * TOK)
-                bank = hpsum.tile([P, PACK, TOK], F32, name="hbank")
-                first_of_half = (c, s) == (0, 0)
-                for t in range(PACK) if first_of_half else reversed(range(PACK)):
-                    nc.tensor.matmul_mx(
-                        out=bank[:, t, :],
-                        lhsT=w1_codes[g][:, t * P : (t + 1) * P].bitcast(FP8X4),
-                        lhsT_scale=w1_scales[g][:, t * P : (t + 1) * P],
-                        rhs=x_codes[:, cols].bitcast(FP8X4),
-                        rhs_scale=x_planes[:].bitcast(U8)[:, cols],
-                        start=True,
-                        stop=True,
-                    )
-                nc.scalar.activation(
-                    h_bf[g][c][:, s * TOK * PACK : (s + 1) * TOK * PACK].rearrange("p (n t) -> p n t", t=PACK),
-                    bank[:].rearrange("p t n -> p n t"),
-                    GELU,
-                    bias=warm_out[:] if (g, c, s) == (0, 0, 0) else 0.0,
-                )
-
-        def quantize_h(g, c):
-            nc.vector.quantize_mx(out=h_codes[g][c][:].bitcast(FP8X4), scales=h_scales[g][c][:], in_=h_bf[g][c][:])
-
-        for c in range(len(CHUNKS)):
-            layer1(0, c)
-
-        w2_codes = keep.tile([P, 2 * N], U32, name="w2_codes", align_bytes=64)
-        w2_scales = keep.tile([P, 2 * N], U8, name="w2_scales", align_bytes=64)
-        group_and_quantize_w1(1, 2)
-        w2_grouped = reuse.tile([P, 2 * N * PACK], BF16, name="w2_grouped", offset=6144, align_bytes=64)
-        nc.vector.tensor_copy(
-            out=w2_grouped[:].rearrange("p (g c i t) -> p g c t i", g=2, i=4, t=PACK),
-            in_=w2_raw[:].rearrange("p g t (c i) -> p g c t i", i=4),
-        )
         quantize_early(0)
         nc.vector.quantize_mx(out=w2_codes[:].bitcast(FP8X4), scales=w2_scales[:], in_=w2_grouped[:])
         quantize_early(1)
 
+        top, bottom = slice(0, HALF), slice(HALF, P)
+        swapped_scales = keep.tile([P, N], U8, name="swapped_scales", align_bytes=64)
+        for i, (dst, src) in enumerate(((top, top), (bottom, bottom), (bottom, top), (top, bottom))):
+            nc.sync.dma_start(masked_codes[:].bitcast(I32)[dst, i * N : (i + 1) * N], w2_codes[:].bitcast(I32)[src, 0:N])
+        for dst, src in ((bottom, top), (top, bottom)):
+            nc.sync.dma_start(swapped_scales[:].bitcast(I32)[dst, :], w2_scales[:].bitcast(I32)[src, 0 : N // 4])
+
+        late_bf = [keep.tile([P, w * PACK], BF16, name="h_bf%d" % c, tag="late%d" % c, align_bytes=64) for c, (a, w) in enumerate(CHUNKS)]
+        late_codes = [keep.tile([P, w], U32, name="h_codes%d" % c, align_bytes=64) for c, (a, w) in enumerate(CHUNKS)]
+        late_scales = [keep.tile([P, w], U8, name="h_scales%d" % c, align_bytes=64) for c, (a, w) in enumerate(CHUNKS)]
+
+        def late_hidden(c):
+            a, w = CHUNKS[c]
+            for s in range(w // TOK):
+                bank = hpsum.tile([P, PACK, TOK], F32, name="hbank")
+                for t in range(PACK) if (c, s) == (0, 0) else reversed(range(PACK)):
+                    hidden_pass(bank[:, t, :], late_w_codes, late_w_scales, slice(t * P, (t + 1) * P), a + s * TOK)
+                gelu(late_bf[c][:, s * TOK * PACK : (s + 1) * TOK * PACK], bank)
+            nc.vector.quantize_mx(out=late_codes[c][:].bitcast(FP8X4), scales=late_scales[c][:], in_=late_bf[c][:])
+
         def layer2(c):
-            w = CHUNKS[c]
+            a, w = CHUNKS[c]
             acc = ypsum.tile([P, w], F32, name="ybank")
-            passes = (0, 1) if c == len(CHUNKS) - 1 else (1, 0)
-            for g in passes:
+            late = [(w2_codes[:, N : 2 * N], w2_scales[:, N : 2 * N], late_codes[c][:], late_scales[c][:])]
+            if a >= FIRST:
+                early = [(w2_codes[:, 0:N], w2_scales[:, 0:N], early_codes[:, a : a + w], early_scales[:, a : a + w])]
+            else:
+                side, b = divmod(a, QUARTER)
+                plane = w2_scales[:, 0:N] if side == 0 else swapped_scales[:]
+                early = [
+                    (
+                        masked_codes[:, (2 * side + q) * N : (2 * side + q + 1) * N],
+                        plane,
+                        early_codes[:, q * QUARTER + b : q * QUARTER + b + w],
+                        early_scales[:, q * QUARTER + b : q * QUARTER + b + w],
+                    )
+                    for q in range(2)
+                ]
+            passes = early + late if a < FIRST else late + early
+            for i, (codes, scales, rhs, rhs_scale) in enumerate(passes):
                 nc.tensor.matmul_mx(
                     out=acc[:],
-                    lhsT=w2_codes[:, g * N : (g + 1) * N].bitcast(FP8X4),
-                    lhsT_scale=w2_scales[:, g * N : (g + 1) * N],
-                    rhs=h_codes[g][c][:].bitcast(FP8X4),
-                    rhs_scale=h_scales[g][c][:],
-                    start=(g == passes[0]),
-                    stop=(g == passes[1]),
+                    lhsT=codes.bitcast(FP8X4),
+                    lhsT_scale=scales,
+                    rhs=rhs.bitcast(FP8X4),
+                    rhs_scale=rhs_scale,
+                    start=(i == 0),
+                    stop=(i == len(passes) - 1),
                 )
             if c >= len(CHUNKS) - 3:
                 y = keep.tile([P, w], F32, name="y%d" % c)
@@ -202,11 +260,10 @@ def tile_picked_pick_mlp_gelu_srt_p_kernel(tc, x_words, x_scales, w1, w2, offs, 
             else:
                 y = keep.tile([P, w], F32, name="y%d" % c, tag="late%d" % (c + 1), align_bytes=64)
                 nc.vector.tensor_copy(y[:], acc[:])
-            nc.sync.dma_start(out[:, starts[c] : starts[c] + w], y[:])
+            nc.sync.dma_start(out[:, a : a + w], y[:])
 
         for c in range(len(CHUNKS)):
-            layer1(1, c)
-            quantize_h(1, c)
+            late_hidden(c)
             if c >= 1:
                 layer2(c - 1)
         layer2(len(CHUNKS) - 1)

@@ -24,7 +24,7 @@ FIRST = 512
 FIRST_WINDOW = T - S + FIRST
 SLOT = 3 * HALF
 CHUNKS = ((512, 256), (768, 256), (0, 256), (256, 128), (384, 128))
-WARM = 4
+WARM = 6
 
 
 def tile_picked_pick_mlp_gelu_srt_p_kernel(tc, x_words, x_scales, w1, w2, offs, out):
@@ -36,11 +36,11 @@ def tile_picked_pick_mlp_gelu_srt_p_kernel(tc, x_words, x_scales, w1, w2, offs, 
         ypsum = ctx.enter_context(tc.psum_pool(name="ypsum", bufs=3))
 
         offsets = keep.tile([P, S // 16], U16, name="offsets")
-        scale_table = reuse.tile([P, T // 4], I32, name="scale_table", offset=4096, align_bytes=64)
-        word_table = reuse.tile([P, T], I32, name="word_table", offset=20480, align_bytes=64)
+        scale_table = reuse.tile([P, T // 4], I32, name="scale_table", offset=12288, align_bytes=64)
+        word_table = reuse.tile([P, T], I32, name="word_table", offset=28672, align_bytes=64)
         quarter_raw = [
             keep.tile([P, PACK, QUARTER], F32, name="quarter_raw0", align_bytes=64),
-            reuse.tile([P, PACK, QUARTER], F32, name="quarter_raw1", offset=512, align_bytes=64),
+            reuse.tile([P, PACK, QUARTER], F32, name="quarter_raw1", offset=8704, align_bytes=64),
         ]
 
         nc.vector.memset(scale_table[0:112, :], 0)
@@ -51,7 +51,7 @@ def tile_picked_pick_mlp_gelu_srt_p_kernel(tc, x_words, x_scales, w1, w2, offs, 
         nc.vector.memset(x_planes[:], 0)
         early_w_codes = keep.tile([P, PACK * SLOT], U32, name="early_w_codes", align_bytes=64)
         early_w_scales = keep.tile([P, PACK * SLOT], U8, name="early_w_scales", align_bytes=64)
-        nc.vector.memset(early_w_codes[:].bitcast(I32), 0)
+        nc.gpsimd.memset(early_w_codes[:].bitcast(I32), 0)
         nc.vector.memset(early_w_scales[:].bitcast(I32), 0)
         w2_scales = keep.tile([P, 2 * N], U8, name="w2_scales", align_bytes=64)
         nc.vector.memset(w2_scales[:].bitcast(I32), 0)
@@ -66,7 +66,7 @@ def tile_picked_pick_mlp_gelu_srt_p_kernel(tc, x_words, x_scales, w1, w2, offs, 
         nc.scalar.activation(warm_out[:], warm_in[:], GELU)
         nc.sync.dma_start(word_table[:, 0:FIRST_WINDOW], words_hbm[:, 0:FIRST_WINDOW])
 
-        picked_scales = reuse.tile([P, S], U8, name="picked_scales", offset=40960, align_bytes=64)
+        picked_scales = reuse.tile([P, S], U8, name="picked_scales", offset=49152, align_bytes=64)
         nc.vector.tensor_copy(picked_scales[:], scale_table[:].bitcast(U8).indirect(offsets[:]))
         for r in range(4):
             nc.sync.dma_start(x_planes[r:P:32, :], picked_scales[:].bitcast(I32)[112 + r : P : 4, :])
@@ -74,21 +74,26 @@ def tile_picked_pick_mlp_gelu_srt_p_kernel(tc, x_words, x_scales, w1, w2, offs, 
         nc.sync.dma_start(word_table[:, FIRST_WINDOW:T], words_hbm[:, FIRST_WINDOW:T])
 
         def group_and_quantize_quarter(q, offset):
-            grouped = reuse.tile([P, QUARTER * PACK], BF16, name="quarter_grouped%d" % q, offset=offset, align_bytes=64)
+            raw = quarter_raw[q][:].rearrange("p j (m t) -> p m j t", t=PACK)
+            pairs = [
+                reuse.tile([P, PASS], BF16, name="pair%d%d" % (q, u), offset=offset + u * 2 * PASS, align_bytes=64)
+                for u in range(2)
+            ]
             for u in range(2):
-                nc.vector.tensor_copy(
-                    out=grouped[:].rearrange("p (t m j) -> p m j t", t=PACK, j=PACK)[:, :, :, 2 * u : 2 * u + 2],
-                    in_=quarter_raw[q][:].rearrange("p j (m t) -> p m j t", t=PACK)[:, :, :, 2 * u : 2 * u + 2],
-                )
+                dst = pairs[u][:].rearrange("p (t m j) -> p m j t", t=2, j=PACK)
+                if (q, u) == (1, 1):
+                    nc.scalar.copy(dst, raw[:, :, :, 2 * u : 2 * u + 2])
+                else:
+                    nc.vector.tensor_copy(out=dst, in_=raw[:, :, :, 2 * u : 2 * u + 2])
             for t in range(PACK):
                 cols = slice(t * SLOT + (q + 1) * HALF, t * SLOT + (q + 2) * HALF)
                 nc.vector.quantize_mx(
                     out=early_w_codes[:, cols].bitcast(FP8X4),
                     scales=early_w_scales[:, cols],
-                    in_=grouped[:, t * HALF * PACK : (t + 1) * HALF * PACK],
+                    in_=pairs[t // 2][:, t % 2 * QUARTER : (t % 2 + 1) * QUARTER],
                 )
 
-        group_and_quantize_quarter(0, 4608)
+        group_and_quantize_quarter(0, 12800)
         warm_bank = ypsum.tile([P, PASS], F32, name="ybank")
         for rep in range(WARM):
             nc.tensor.matmul_mx(
@@ -100,11 +105,11 @@ def tile_picked_pick_mlp_gelu_srt_p_kernel(tc, x_words, x_scales, w1, w2, offs, 
                 start=True,
                 stop=True,
             )
-        masked_codes = reuse.tile([P, 4 * N], U32, name="masked_codes", offset=4608, align_bytes=64)
+        masked_codes = reuse.tile([P, 4 * N], U32, name="masked_codes", offset=12800, align_bytes=64)
         nc.vector.memset(masked_codes[:].bitcast(I32), 0)
 
-        late_raw = reuse.tile([P, PACK, PASS], F32, name="late_raw", offset=7680, align_bytes=64)
-        w2_raw = reuse.tile([P, 2, PACK, N], F32, name="w2_raw", offset=41472, align_bytes=64)
+        late_raw = reuse.tile([P, PACK, PASS], F32, name="late_raw", offset=15872, align_bytes=64)
+        w2_raw = reuse.tile([P, 2, PACK, N], F32, name="w2_raw", offset=49664, align_bytes=64)
         for q in range(2):
             nc.sync.dma_start(
                 late_raw[:, :, q * QUARTER : (q + 1) * QUARTER],
@@ -116,8 +121,8 @@ def tile_picked_pick_mlp_gelu_srt_p_kernel(tc, x_words, x_scales, w1, w2, offs, 
         nc.vector.tensor_copy(
             x_first[:], word_table[:, 0:FIRST_WINDOW].bitcast(U32).indirect(offsets[:, 0 : FIRST // 16])
         )
-        group_and_quantize_quarter(1, 16384)
-        x_rest = reuse.tile([P, S - FIRST], U32, name="x_rest", offset=16384, align_bytes=64)
+        group_and_quantize_quarter(1, 24576)
+        x_rest = reuse.tile([P, S - FIRST], U32, name="x_rest", offset=24576, align_bytes=64)
         nc.vector.tensor_copy(x_rest[:], word_table[:].bitcast(U32).indirect(offsets[:, FIRST // 16 : S // 16]))
 
         def tokens(a):
@@ -144,9 +149,9 @@ def tile_picked_pick_mlp_gelu_srt_p_kernel(tc, x_words, x_scales, w1, w2, offs, 
                 bias=warm_out[:] if first else 0.0,
             )
 
-        early_bf = keep.tile([P, S * PACK], BF16, name="early_bf", align_bytes=64)
+        early_bf = reuse.tile([P, S * PACK], BF16, name="early_bf", offset=4608, align_bytes=64)
         early_codes = keep.tile([P, S], U32, name="early_codes", align_bytes=64)
-        early_scales = reuse.tile([P, S], U8, name="early_scales", offset=22528, align_bytes=64)
+        early_scales = reuse.tile([P, S], U8, name="early_scales", offset=31744, align_bytes=64)
 
         for q in range(2):
             for s in range(2):
@@ -170,28 +175,37 @@ def tile_picked_pick_mlp_gelu_srt_p_kernel(tc, x_words, x_scales, w1, w2, offs, 
 
         late_w_codes = keep.tile([P, PASS], U32, name="late_w_codes", align_bytes=64)
         late_w_scales = keep.tile([P, PASS], U8, name="late_w_scales", align_bytes=64)
-        late_grouped = reuse.tile([P, PASS * PACK], BF16, name="late_grouped", offset=20480, align_bytes=64)
         for q in range(2):
-            ms = slice(q * HALF, (q + 1) * HALF)
+            raw = late_raw[:, :, q * QUARTER : (q + 1) * QUARTER].rearrange("p j (m t) -> p m j t", t=PACK)
+            grouped = reuse.tile(
+                [P, QUARTER * PACK], BF16, name="late_grouped%d" % q, offset=28672 + q * 2048, align_bytes=64
+            )
             for u in range(2):
                 nc.vector.tensor_copy(
-                    out=late_grouped[:].rearrange("p (t m j) -> p m j t", t=PACK, j=PACK)[:, ms, :, 2 * u : 2 * u + 2],
-                    in_=late_raw[:].rearrange("p j (m t) -> p m j t", t=PACK)[:, ms, :, 2 * u : 2 * u + 2],
+                    out=grouped[:].rearrange("p (t m j) -> p m j t", t=PACK, j=PACK)[:, :, :, 2 * u : 2 * u + 2],
+                    in_=raw[:, :, :, 2 * u : 2 * u + 2],
                 )
-        for u in range(2):
-            cols = slice(u * 2 * P, (u + 1) * 2 * P)
-            nc.vector.quantize_mx(
-                out=late_w_codes[:, cols].bitcast(FP8X4),
-                scales=late_w_scales[:, cols],
-                in_=late_grouped[:, u * 2 * P * PACK : (u + 1) * 2 * P * PACK],
-            )
+            for t in range(PACK):
+                cols = slice(t * P + q * HALF, t * P + (q + 1) * HALF)
+                nc.vector.quantize_mx(
+                    out=late_w_codes[:, cols].bitcast(FP8X4),
+                    scales=late_w_scales[:, cols],
+                    in_=grouped[:, t * QUARTER : (t + 1) * QUARTER],
+                )
 
         w2_codes = keep.tile([P, 2 * N], U32, name="w2_codes", align_bytes=64)
-        w2_grouped = reuse.tile([P, 2 * N * PACK], BF16, name="w2_grouped", offset=20480, align_bytes=64)
-        nc.vector.tensor_copy(
-            out=w2_grouped[:].rearrange("p (g c i t) -> p g c t i", g=2, i=4, t=PACK),
-            in_=w2_raw[:].rearrange("p g t (c i) -> p g c t i", i=4),
-        )
+        w2_grouped = reuse.tile([P, 2 * N * PACK], BF16, name="w2_grouped", offset=29696, align_bytes=64)
+        for g in range(2):
+            nc.vector.tensor_copy(
+                out=w2_grouped[:, g * PASS : (g + 1) * PASS].rearrange("p (c i t) -> p c t i", i=4, t=PACK),
+                in_=w2_raw[:, g, :, :].rearrange("p t (c i) -> p c t i", i=4),
+            )
+        for g in range(2):
+            nc.vector.quantize_mx(
+                out=w2_codes[:, g * N : (g + 1) * N].bitcast(FP8X4),
+                scales=w2_scales[:, g * N : (g + 1) * N],
+                in_=w2_grouped[:, g * PASS : (g + 1) * PASS],
+            )
 
         def quantize_early(half):
             cols = slice(half * S // 2, (half + 1) * S // 2)
@@ -202,7 +216,6 @@ def tile_picked_pick_mlp_gelu_srt_p_kernel(tc, x_words, x_scales, w1, w2, offs, 
             )
 
         quantize_early(0)
-        nc.vector.quantize_mx(out=w2_codes[:].bitcast(FP8X4), scales=w2_scales[:], in_=w2_grouped[:])
         quantize_early(1)
 
         top, bottom = slice(0, HALF), slice(HALF, P)

@@ -215,7 +215,6 @@ def tile_picked_pick_mlp_gelu_srt_p_kernel(tc, x_words, x_scales, w1, w2, offs, 
                 in_=early_bf[:, half * S // 2 * PACK : (half + 1) * S // 2 * PACK],
             )
 
-        quantize_early(0)
         quantize_early(1)
 
         top, bottom = slice(0, HALF), slice(HALF, P)
@@ -271,12 +270,14 @@ def tile_picked_pick_mlp_gelu_srt_p_kernel(tc, x_words, x_scales, w1, w2, offs, 
                 y = keep.tile([P, w], F32, name="y%d" % c)
                 nc.scalar.copy(y[:], acc[:])
             else:
-                y = keep.tile([P, w], F32, name="y%d" % c, tag="late%d" % (c + 1), align_bytes=64)
+                y = keep.tile([P, w], F32, name="y%d" % c, tag="late%d" % (1 - c), align_bytes=64)
                 nc.vector.tensor_copy(y[:], acc[:])
             nc.sync.dma_start(out[:, a : a + w], y[:])
 
         for c in range(len(CHUNKS)):
             late_hidden(c)
+            if c == 0:
+                quantize_early(0)
             if c >= 1:
                 layer2(c - 1)
         layer2(len(CHUNKS) - 1)

@@ -38,9 +38,10 @@ def tile_picked_pick_mlp_gelu_srt_p_kernel(tc, x_words, x_scales, w1, w2, offs, 
         offsets = keep.tile([P, S // 16], U16, name="offsets")
         scale_table = reuse.tile([P, T // 4], I32, name="scale_table", offset=12288, align_bytes=64)
         word_table = reuse.tile([P, T], I32, name="word_table", offset=28672, align_bytes=64)
-        quarter_raw = [
-            keep.tile([P, PACK, QUARTER], F32, name="quarter_raw0", align_bytes=64),
-            reuse.tile([P, PACK, QUARTER], F32, name="quarter_raw1", offset=8704, align_bytes=64),
+        quarter_raw = keep.tile([P, PACK, QUARTER], F32, name="quarter_raw0", align_bytes=64)
+        eighth_raw = [
+            reuse.tile([P, PACK, P], F32, name="eighth_raw%d" % e, offset=(10752, 14848)[e], align_bytes=64)
+            for e in range(2)
         ]
 
         nc.vector.memset(scale_table[0:112, :], 0)
@@ -61,30 +62,35 @@ def tile_picked_pick_mlp_gelu_srt_p_kernel(tc, x_words, x_scales, w1, w2, offs, 
         w1_hbm = w1.rearrange("(p j) c -> p j c", j=PACK)
 
         nc.sync.dma_start(offsets[:], offs)
-        nc.sync.dma_start(quarter_raw[0][:], w1_hbm[:, :, 0:QUARTER])
+        nc.sync.dma_start(quarter_raw[:], w1_hbm[:, :, 0:QUARTER])
         nc.scalar.dma_start(scale_table[112:P, :], scales_hbm)
         nc.scalar.activation(warm_out[:], warm_in[:], GELU)
         nc.sync.dma_start(word_table[:, 0:FIRST_WINDOW], words_hbm[:, 0:FIRST_WINDOW])
 
-        picked_scales = reuse.tile([P, S], U8, name="picked_scales", offset=49152, align_bytes=64)
+        picked_scales = reuse.tile([P, S], U8, name="picked_scales", offset=53248, align_bytes=64)
         nc.vector.tensor_copy(picked_scales[:], scale_table[:].bitcast(U8).indirect(offsets[:]))
         for r in range(4):
             nc.sync.dma_start(x_planes[r:P:32, :], picked_scales[:].bitcast(I32)[112 + r : P : 4, :])
-        nc.sync.dma_start(quarter_raw[1][:], w1_hbm[:, :, QUARTER:PASS])
+        for e in range(2):
+            nc.sync.dma_start(eighth_raw[e][:], w1_hbm[:, :, QUARTER + e * P : QUARTER + (e + 1) * P])
         nc.sync.dma_start(word_table[:, FIRST_WINDOW:T], words_hbm[:, FIRST_WINDOW:T])
 
         def group_and_quantize_quarter(q, offset):
-            raw = quarter_raw[q][:].rearrange("p j (m t) -> p m j t", t=PACK)
             pairs = [
                 reuse.tile([P, PASS], BF16, name="pair%d%d" % (q, u), offset=offset + u * 2 * PASS, align_bytes=64)
                 for u in range(2)
             ]
-            for u in range(2):
-                dst = pairs[u][:].rearrange("p (t m j) -> p m j t", t=2, j=PACK)
-                if (q, u) == (1, 1):
-                    nc.scalar.copy(dst, raw[:, :, :, 2 * u : 2 * u + 2])
-                else:
-                    nc.vector.tensor_copy(out=dst, in_=raw[:, :, :, 2 * u : 2 * u + 2])
+            dst = [pairs[u][:].rearrange("p (t m j) -> p m j t", t=2, j=PACK) for u in range(2)]
+            if q == 0:
+                raw = quarter_raw[:].rearrange("p j (m t) -> p m j t", t=PACK)
+                for u in range(2):
+                    nc.vector.tensor_copy(out=dst[u], in_=raw[:, :, :, 2 * u : 2 * u + 2])
+            else:
+                raw = [eighth_raw[e][:].rearrange("p j (m t) -> p m j t", t=PACK) for e in range(2)]
+                for u in range(2):
+                    nc.scalar.copy(dst[u][:, 0:32], raw[0][:, :, :, 2 * u : 2 * u + 2])
+                for u in range(2):
+                    nc.vector.tensor_copy(out=dst[u][:, 32:64], in_=raw[1][:, :, :, 2 * u : 2 * u + 2])
             for t in range(PACK):
                 cols = slice(t * SLOT + (q + 1) * HALF, t * SLOT + (q + 2) * HALF)
                 nc.vector.quantize_mx(
@@ -108,13 +114,11 @@ def tile_picked_pick_mlp_gelu_srt_p_kernel(tc, x_words, x_scales, w1, w2, offs, 
         masked_codes = reuse.tile([P, 4 * N], U32, name="masked_codes", offset=12800, align_bytes=64)
         nc.vector.memset(masked_codes[:].bitcast(I32), 0)
 
-        late_raw = reuse.tile([P, PACK, PASS], F32, name="late_raw", offset=15872, align_bytes=64)
-        w2_raw = reuse.tile([P, 2, PACK, N], F32, name="w2_raw", offset=49664, align_bytes=64)
-        for q in range(2):
-            nc.sync.dma_start(
-                late_raw[:, :, q * QUARTER : (q + 1) * QUARTER],
-                w1_hbm[:, :, PASS + q * QUARTER : PASS + (q + 1) * QUARTER],
-            )
+        late_raw = reuse.tile([P, PACK, PASS], F32, name="late_raw", offset=45120, align_bytes=64)
+        w2_raw = reuse.tile([P, 2, PACK, N], F32, name="w2_raw", offset=53760, align_bytes=64)
+        pieces = ((0, QUARTER), (QUARTER, P), (QUARTER + P, P))
+        for a, w in pieces:
+            nc.sync.dma_start(late_raw[:, :, a : a + w], w1_hbm[:, :, PASS + a : PASS + a + w])
         nc.sync.dma_start(w2_raw[:], w2.rearrange("(g p t) n -> p g t n", g=2, t=PACK))
 
         x_first = keep.tile([P, FIRST], U32, name="x_first", align_bytes=64)
@@ -176,15 +180,17 @@ def tile_picked_pick_mlp_gelu_srt_p_kernel(tc, x_words, x_scales, w1, w2, offs, 
         late_w_codes = keep.tile([P, PASS], U32, name="late_w_codes", align_bytes=64)
         late_w_scales = keep.tile([P, PASS], U8, name="late_w_scales", align_bytes=64)
         for q in range(2):
-            raw = late_raw[:, :, q * QUARTER : (q + 1) * QUARTER].rearrange("p j (m t) -> p m j t", t=PACK)
             grouped = reuse.tile(
                 [P, QUARTER * PACK], BF16, name="late_grouped%d" % q, offset=28672 + q * 2048, align_bytes=64
             )
-            for u in range(2):
-                nc.vector.tensor_copy(
-                    out=grouped[:].rearrange("p (t m j) -> p m j t", t=PACK, j=PACK)[:, :, :, 2 * u : 2 * u + 2],
-                    in_=raw[:, :, :, 2 * u : 2 * u + 2],
-                )
+            for a, w in pieces[:1] if q == 0 else pieces[1:]:
+                raw = late_raw[:, :, a : a + w].rearrange("p j (m t) -> p m j t", t=PACK)
+                rows = slice(a % QUARTER // PACK, (a % QUARTER + w) // PACK)
+                for u in range(2):
+                    nc.vector.tensor_copy(
+                        out=grouped[:].rearrange("p (t m j) -> p m j t", t=PACK, j=PACK)[:, rows, :, 2 * u : 2 * u + 2],
+                        in_=raw[:, :, :, 2 * u : 2 * u + 2],
+                    )
             for t in range(PACK):
                 cols = slice(t * P + q * HALF, t * P + (q + 1) * HALF)
                 nc.vector.quantize_mx(
@@ -220,7 +226,8 @@ def tile_picked_pick_mlp_gelu_srt_p_kernel(tc, x_words, x_scales, w1, w2, offs, 
         top, bottom = slice(0, HALF), slice(HALF, P)
         swapped_scales = keep.tile([P, N], U8, name="swapped_scales", align_bytes=64)
         for i, (dst, src) in enumerate(((top, top), (bottom, bottom), (bottom, top), (top, bottom))):
-            nc.sync.dma_start(masked_codes[:].bitcast(I32)[dst, i * N : (i + 1) * N], w2_codes[:].bitcast(I32)[src, 0:N])
+            move = nc.vector.tensor_copy if i < 2 else nc.sync.dma_start
+            move(masked_codes[:].bitcast(I32)[dst, i * N : (i + 1) * N], w2_codes[:].bitcast(I32)[src, 0:N])
         for dst, src in ((bottom, top), (top, bottom)):
             nc.sync.dma_start(swapped_scales[:].bitcast(I32)[dst, :], w2_scales[:].bitcast(I32)[src, 0 : N // 4])
 

@@ -36,7 +36,7 @@ def tile_picked_pick_mlp_gelu_srt_p_kernel(tc, x_words, x_scales, w1, w2, offs, 
         ypsum = ctx.enter_context(tc.psum_pool(name="ypsum", bufs=3))
 
         offsets = keep.tile([P, S // 16], U16, name="offsets")
-        scale_table = reuse.tile([P, T // 4], I32, name="scale_table", offset=12288, align_bytes=64)
+        scale_table = reuse.tile([P, T // 4 + 320], I32, name="scale_table", offset=12288, align_bytes=64)
         word_table = reuse.tile([P, T], I32, name="word_table", offset=28672, align_bytes=64)
         quarter_raw = keep.tile([P, PACK, QUARTER], F32, name="quarter_raw0", align_bytes=64)
         eighth_raw = [
@@ -44,16 +44,14 @@ def tile_picked_pick_mlp_gelu_srt_p_kernel(tc, x_words, x_scales, w1, w2, offs, 
             for e in range(2)
         ]
 
-        nc.vector.memset(scale_table[0:112, :], 0)
+        nc.vector.memset(scale_table[0:112, 0 : T // 4], 0)
         warm_in = keep.tile([P, 1], F32, name="warm_in")
         warm_out = keep.tile([P, 1], F32, name="warm_out")
         nc.vector.memset(warm_in[:], 0.0)
         x_planes = keep.tile([P, S // 4], I32, name="x_planes", align_bytes=64)
         nc.vector.memset(x_planes[:], 0)
         early_w_codes = keep.tile([P, PACK * SLOT], U32, name="early_w_codes", align_bytes=64)
-        early_w_scales = keep.tile([P, PACK * SLOT], U8, name="early_w_scales", align_bytes=64)
         nc.gpsimd.memset(early_w_codes[:].bitcast(I32), 0)
-        nc.vector.memset(early_w_scales[:].bitcast(I32), 0)
         w2_scales = keep.tile([P, 2 * N], U8, name="w2_scales", align_bytes=64)
         nc.vector.memset(w2_scales[:].bitcast(I32), 0)
 
@@ -63,12 +61,14 @@ def tile_picked_pick_mlp_gelu_srt_p_kernel(tc, x_words, x_scales, w1, w2, offs, 
 
         nc.sync.dma_start(offsets[:], offs)
         nc.sync.dma_start(quarter_raw[:], w1_hbm[:, :, 0:QUARTER])
-        nc.scalar.dma_start(scale_table[112:P, :], scales_hbm)
+        nc.scalar.dma_start(scale_table[112:P, 0 : T // 4], scales_hbm)
         nc.scalar.activation(warm_out[:], warm_in[:], GELU)
         nc.sync.dma_start(word_table[:, 0:FIRST_WINDOW], words_hbm[:, 0:FIRST_WINDOW])
 
         picked_scales = reuse.tile([P, S], U8, name="picked_scales", offset=53248, align_bytes=64)
-        nc.vector.tensor_copy(picked_scales[:], scale_table[:].bitcast(U8).indirect(offsets[:]))
+        nc.vector.tensor_copy(picked_scales[:], scale_table[:, 0 : T // 4].bitcast(U8).indirect(offsets[:]))
+        early_w_scales = reuse.tile([P, PACK * SLOT], U8, name="early_w_scales", offset=16896, align_bytes=64)
+        nc.vector.memset(early_w_scales[:].bitcast(I32).rearrange("p (t s w) -> p t s w", t=PACK, s=3)[:, :, 0:3:2, :], 0)
         for r in range(4):
             nc.sync.dma_start(x_planes[r:P:32, :], picked_scales[:].bitcast(I32)[112 + r : P : 4, :])
         for e in range(2):
@@ -84,14 +84,14 @@ def tile_picked_pick_mlp_gelu_srt_p_kernel(tc, x_words, x_scales, w1, w2, offs, 
             if q == 0:
                 raw = quarter_raw[:].rearrange("p j (m t) -> p m j t", t=PACK)
                 for u in range(2):
-                    nc.vector.tensor_copy(out=dst[u], in_=raw[:, :, :, 2 * u : 2 * u + 2])
+                    nc.scalar.copy(dst[u], raw[:, :, :, 2 * u : 2 * u + 2])
             else:
                 raw = [eighth_raw[e][:].rearrange("p j (m t) -> p m j t", t=PACK) for e in range(2)]
                 for u in range(2):
                     nc.scalar.copy(dst[u][:, 0:32], raw[0][:, :, :, 2 * u : 2 * u + 2])
                 for u in range(2):
                     nc.vector.tensor_copy(out=dst[u][:, 32:64], in_=raw[1][:, :, :, 2 * u : 2 * u + 2])
-            for t in range(PACK):
+            for t in (1, 2, 0, 3) if q == 0 else range(PACK):
                 cols = slice(t * SLOT + (q + 1) * HALF, t * SLOT + (q + 2) * HALF)
                 nc.vector.quantize_mx(
                     out=early_w_codes[:, cols].bitcast(FP8X4),
@@ -99,19 +99,19 @@ def tile_picked_pick_mlp_gelu_srt_p_kernel(tc, x_words, x_scales, w1, w2, offs, 
                     in_=pairs[t // 2][:, t % 2 * QUARTER : (t % 2 + 1) * QUARTER],
                 )
 
-        group_and_quantize_quarter(0, 12800)
+        group_and_quantize_quarter(0, 0)
         warm_bank = ypsum.tile([P, PASS], F32, name="ybank")
         for rep in range(WARM):
             nc.tensor.matmul_mx(
                 out=warm_bank[0:32, :],
-                lhsT=early_w_codes[:, HALF : HALF + 32].bitcast(FP8X4),
-                lhsT_scale=early_w_scales[:, HALF : HALF + 32],
-                rhs=early_w_codes[:, QUARTER : QUARTER + PASS].bitcast(FP8X4),
-                rhs_scale=early_w_scales[:, QUARTER : QUARTER + PASS],
+                lhsT=early_w_codes[:, QUARTER : QUARTER + 32].bitcast(FP8X4),
+                lhsT_scale=early_w_scales[:, QUARTER : QUARTER + 32],
+                rhs=early_w_codes[:, P : P + PASS].bitcast(FP8X4),
+                rhs_scale=early_w_scales[:, P : P + PASS],
                 start=True,
                 stop=True,
             )
-        masked_codes = reuse.tile([P, 4 * N], U32, name="masked_codes", offset=12800, align_bytes=64)
+        masked_codes = reuse.tile([P, 4 * N], U32, name="masked_codes", offset=0, align_bytes=64)
         nc.vector.memset(masked_codes[:].bitcast(I32), 0)
 
         late_raw = reuse.tile([P, PACK, PASS], F32, name="late_raw", offset=45120, align_bytes=64)

@@ -165,9 +165,7 @@ def tile_picked_pick_mlp_gelu_srt_p_kernel(tc, x_words, x_scales, w1, w2, offs, 
                 for t in order:
                     a = t * SLOT + q * HALF
                     hidden_pass(bank[:, t, :], early_w_codes, early_w_scales, slice(a, a + P), lower)
-                for t in order:
-                    a = t * SLOT + (q + 1) * HALF
-                    hidden_pass(bank[0:HALF, t, :], early_w_codes, early_w_scales, slice(a, a + HALF), upper)
+                    hidden_pass(bank[0:HALF, t, :], early_w_codes, early_w_scales, slice(a + HALF, a + P), upper)
                 at = (q * QUARTER + s * TOK) * PACK
                 gelu(early_bf[:, at : at + TOK * PACK], bank, first=(q, s) == (0, 0))
         for a in range(FIRST, S, TOK):

@@ -35,12 +35,12 @@ def tile_picked_pick_mlp_gelu_srt_p_kernel(tc, x_words, x_scales, w1, w2, offs, 
         hpsum = ctx.enter_context(tc.psum_pool(name="hpsum", bufs=5))
         ypsum = ctx.enter_context(tc.psum_pool(name="ypsum", bufs=3))
 
-        offsets = keep.tile([P, S // 16], U16, name="offsets")
-        scale_table = reuse.tile([P, T // 4 + 320], I32, name="scale_table", offset=12288, align_bytes=64)
-        word_table = reuse.tile([P, T], I32, name="word_table", offset=28672, align_bytes=64)
-        quarter_raw = keep.tile([P, PACK, QUARTER], F32, name="quarter_raw0", align_bytes=64)
+        offsets = keep.tile([P, S // 16], U16, name="offsets", align_bytes=256)
+        scale_table = reuse.tile([P, T // 4 + 320], I32, name="scale_table", offset=12288, align_bytes=256)
+        word_table = reuse.tile([P, T], I32, name="word_table", offset=28672, align_bytes=256)
+        quarter_raw = keep.tile([P, PACK, QUARTER], F32, name="quarter_raw0", align_bytes=256)
         eighth_raw = [
-            reuse.tile([P, PACK, P], F32, name="eighth_raw%d" % e, offset=(10752, 14848)[e], align_bytes=64)
+            reuse.tile([P, PACK, P], F32, name="eighth_raw%d" % e, offset=(10752, 14848)[e], align_bytes=256)
             for e in range(2)
         ]
 
@@ -48,11 +48,11 @@ def tile_picked_pick_mlp_gelu_srt_p_kernel(tc, x_words, x_scales, w1, w2, offs, 
         warm_in = keep.tile([P, 1], F32, name="warm_in")
         warm_out = keep.tile([P, 1], F32, name="warm_out")
         nc.vector.memset(warm_in[:], 0.0)
-        x_planes = keep.tile([P, S // 4], I32, name="x_planes", align_bytes=64)
+        x_planes = keep.tile([P, S // 4], I32, name="x_planes", align_bytes=256)
         nc.vector.memset(x_planes[:], 0)
         early_w_codes = keep.tile([P, PACK * SLOT], U32, name="early_w_codes", align_bytes=64)
         nc.gpsimd.memset(early_w_codes[:].bitcast(I32), 0)
-        w2_scales = keep.tile([P, 2 * N], U8, name="w2_scales", align_bytes=64)
+        w2_scales = keep.tile([P, 2 * N], U8, name="w2_scales", align_bytes=256)
         nc.vector.memset(w2_scales[:].bitcast(I32), 0)
 
         words_hbm = x_words[0].rearrange("p c r -> p (c r)").bitcast(I32)
@@ -65,7 +65,7 @@ def tile_picked_pick_mlp_gelu_srt_p_kernel(tc, x_words, x_scales, w1, w2, offs, 
         nc.scalar.activation(warm_out[:], warm_in[:], GELU)
         nc.sync.dma_start(word_table[:, 0:FIRST_WINDOW], words_hbm[:, 0:FIRST_WINDOW])
 
-        picked_scales = reuse.tile([P, S], U8, name="picked_scales", offset=53248, align_bytes=64)
+        picked_scales = reuse.tile([P, S], U8, name="picked_scales", offset=52992, align_bytes=256)
         nc.vector.tensor_copy(picked_scales[:], scale_table[:, 0 : T // 4].bitcast(U8).indirect(offsets[:]))
         early_w_scales = reuse.tile([P, PACK * SLOT], U8, name="early_w_scales", offset=16896, align_bytes=64)
         nc.vector.memset(early_w_scales[:].bitcast(I32).rearrange("p (t s w) -> p t s w", t=PACK, s=3)[:, :, 0:3:2, :], 0)
@@ -111,11 +111,11 @@ def tile_picked_pick_mlp_gelu_srt_p_kernel(tc, x_words, x_scales, w1, w2, offs, 
                 start=True,
                 stop=True,
             )
-        masked_codes = reuse.tile([P, 4 * N], U32, name="masked_codes", offset=0, align_bytes=64)
+        masked_codes = reuse.tile([P, 4 * N], U32, name="masked_codes", offset=0, align_bytes=256)
         nc.vector.memset(masked_codes[:].bitcast(I32), 0)
 
-        late_raw = reuse.tile([P, PACK, PASS], F32, name="late_raw", offset=45120, align_bytes=64)
-        w2_raw = reuse.tile([P, 2, PACK, N], F32, name="w2_raw", offset=53760, align_bytes=64)
+        late_raw = reuse.tile([P, PACK, PASS], F32, name="late_raw", offset=45056, align_bytes=256)
+        w2_raw = reuse.tile([P, 2, PACK, N], F32, name="w2_raw", offset=53760, align_bytes=256)
         pieces = ((0, QUARTER), (QUARTER, P), (QUARTER + P, P))
         for a, w in pieces:
             nc.sync.dma_start(late_raw[:, :, a : a + w], w1_hbm[:, :, PASS + a : PASS + a + w])
@@ -197,7 +197,7 @@ def tile_picked_pick_mlp_gelu_srt_p_kernel(tc, x_words, x_scales, w1, w2, offs, 
                     in_=grouped[:, t * QUARTER : (t + 1) * QUARTER],
                 )
 
-        w2_codes = keep.tile([P, 2 * N], U32, name="w2_codes", align_bytes=64)
+        w2_codes = keep.tile([P, 2 * N], U32, name="w2_codes", align_bytes=256)
         w2_grouped = reuse.tile([P, 2 * N * PACK], BF16, name="w2_grouped", offset=29696, align_bytes=64)
         for g in range(2):
             nc.vector.tensor_copy(
@@ -222,14 +222,14 @@ def tile_picked_pick_mlp_gelu_srt_p_kernel(tc, x_words, x_scales, w1, w2, offs, 
         quantize_early(1)
 
         top, bottom = slice(0, HALF), slice(HALF, P)
-        swapped_scales = keep.tile([P, N], U8, name="swapped_scales", align_bytes=64)
+        swapped_scales = keep.tile([P, N], U8, name="swapped_scales", align_bytes=256)
         for i, (dst, src) in enumerate(((top, top), (bottom, bottom), (bottom, top), (top, bottom))):
             move = nc.vector.tensor_copy if i < 2 else nc.sync.dma_start
             move(masked_codes[:].bitcast(I32)[dst, i * N : (i + 1) * N], w2_codes[:].bitcast(I32)[src, 0:N])
         for dst, src in ((bottom, top), (top, bottom)):
             nc.sync.dma_start(swapped_scales[:].bitcast(I32)[dst, :], w2_scales[:].bitcast(I32)[src, 0 : N // 4])
 
-        late_bf = [keep.tile([P, w * PACK], BF16, name="h_bf%d" % c, tag="late%d" % c, align_bytes=64) for c, (a, w) in enumerate(CHUNKS)]
+        late_bf = [keep.tile([P, w * PACK], BF16, name="h_bf%d" % c, tag="late%d" % c, align_bytes=256) for c, (a, w) in enumerate(CHUNKS)]
         late_codes = [keep.tile([P, w], U32, name="h_codes%d" % c, align_bytes=64) for c, (a, w) in enumerate(CHUNKS)]
         late_scales = [keep.tile([P, w], U8, name="h_scales%d" % c, align_bytes=64) for c, (a, w) in enumerate(CHUNKS)]
 
@@ -272,10 +272,10 @@ def tile_picked_pick_mlp_gelu_srt_p_kernel(tc, x_words, x_scales, w1, w2, offs, 
                     stop=(i == len(passes) - 1),
                 )
             if c >= len(CHUNKS) - 3:
-                y = keep.tile([P, w], F32, name="y%d" % c)
+                y = keep.tile([P, w], F32, name="y%d" % c, align_bytes=256)
                 nc.scalar.copy(y[:], acc[:])
             else:
-                y = keep.tile([P, w], F32, name="y%d" % c, tag="late%d" % (1 - c), align_bytes=64)
+                y = keep.tile([P, w], F32, name="y%d" % c, tag="late%d" % (1 - c), align_bytes=256)
                 nc.vector.tensor_copy(y[:], acc[:])
             nc.sync.dma_start(out[:, a : a + w], y[:])
 

from contextlib import ExitStack

import concourse.mybir as mybir

K, T, S, H, N = 512, 4096, 1024, 1024, 128
FLOPS = 2 * S * (K * H + H * N)

F32 = mybir.dt.float32
BF16 = mybir.dt.bfloat16
I32 = mybir.dt.int32
U32 = mybir.dt.uint32
U16 = mybir.dt.uint16
U8 = mybir.dt.uint8
FP8X4 = mybir.dt.float8_e4m3fn_x4
GELU = mybir.ActivationFunctionType.Gelu_apprx_tanh

P = 128
HALF = 64
PACK = 4
PASS = P * PACK
QUARTER = 256
TOK = 128
FIRST = 512
FIRST_WINDOW = T - S + FIRST
SLOT = 3 * HALF
CHUNKS = ((512, 256), (768, 256), (0, 256), (256, 128), (384, 128))
WARM = 6


def tile_picked_pick_mlp_gelu_srt_p_kernel(tc, x_words, x_scales, w1, w2, offs, out):
    nc = tc.nc
    with ExitStack() as ctx:
        keep = ctx.enter_context(tc.tile_pool(name="keep", bufs=1))
        reuse = ctx.enter_context(tc.tile_pool(name="reuse", bufs=1))
        hpsum = ctx.enter_context(tc.psum_pool(name="hpsum", bufs=5))
        ypsum = ctx.enter_context(tc.psum_pool(name="ypsum", bufs=3))

        offsets = keep.tile([P, S // 16], U16, name="offsets", align_bytes=256)
        scale_table = reuse.tile([P, T // 4 + 320], I32, name="scale_table", offset=12288, align_bytes=256)
        word_table = reuse.tile([P, T], I32, name="word_table", offset=28672, align_bytes=256)
        quarter_raw = keep.tile([P, PACK, QUARTER], F32, name="quarter_raw0", align_bytes=256)
        eighth_raw = [
            reuse.tile([P, PACK, P], F32, name="eighth_raw%d" % e, offset=(10752, 14848)[e], align_bytes=256)
            for e in range(2)
        ]

        nc.vector.memset(scale_table[0:112, 0 : T // 4], 0)
        warm_in = keep.tile([P, 1], F32, name="warm_in")
        warm_out = keep.tile([P, 1], F32, name="warm_out")
        nc.vector.memset(warm_in[:], 0.0)
        x_planes = keep.tile([P, S // 4], I32, name="x_planes", align_bytes=256)
        nc.vector.memset(x_planes[:], 0)
        early_w_codes = keep.tile([P, PACK * SLOT], U32, name="early_w_codes", align_bytes=64)
        nc.gpsimd.memset(early_w_codes[:].bitcast(I32), 0)
        w2_scales = keep.tile([P, 2 * N], U8, name="w2_scales", align_bytes=256)
        nc.vector.memset(w2_scales[:].bitcast(I32), 0)

        words_hbm = x_words[0].rearrange("p c r -> p (c r)").bitcast(I32)
        scales_hbm = x_scales[0].bitcast(I32)
        w1_hbm = w1.rearrange("(p j) c -> p j c", j=PACK)

        nc.sync.dma_start(offsets[:], offs)
        nc.sync.dma_start(quarter_raw[:], w1_hbm[:, :, 0:QUARTER])
        nc.scalar.dma_start(scale_table[112:P, 0 : T // 4], scales_hbm)
        nc.scalar.activation(warm_out[:], warm_in[:], GELU)
        nc.sync.dma_start(word_table[:, 0:FIRST_WINDOW], words_hbm[:, 0:FIRST_WINDOW])

        picked_scales = reuse.tile([P, S], U8, name="picked_scales", offset=52992, align_bytes=256)
        nc.vector.tensor_copy(picked_scales[:], scale_table[:, 0 : T // 4].bitcast(U8).indirect(offsets[:]))
        early_w_scales = reuse.tile([P, PACK * SLOT], U8, name="early_w_scales", offset=16896, align_bytes=64)
        nc.vector.memset(early_w_scales[:].bitcast(I32).rearrange("p (t s w) -> p t s w", t=PACK, s=3)[:, :, 0:3:2, :], 0)
        for r in range(4):
            nc.sync.dma_start(x_planes[r:P:32, :], picked_scales[:].bitcast(I32)[112 + r : P : 4, :])
        for e in range(2):
            nc.sync.dma_start(eighth_raw[e][:], w1_hbm[:, :, QUARTER + e * P : QUARTER + (e + 1) * P])
        nc.sync.dma_start(word_table[:, FIRST_WINDOW:T], words_hbm[:, FIRST_WINDOW:T])

        def group_and_quantize_quarter(q, offset):
            pairs = [
                reuse.tile([P, PASS], BF16, name="pair%d%d" % (q, u), offset=offset + u * 2 * PASS, align_bytes=64)
                for u in range(2)
            ]
            dst = [pairs[u][:].rearrange("p (t m j) -> p m j t", t=2, j=PACK) for u in range(2)]
            if q == 0:
                raw = quarter_raw[:].rearrange("p j (m t) -> p m j t", t=PACK)
                for u in range(2):
                    nc.scalar.copy(dst[u], raw[:, :, :, 2 * u : 2 * u + 2])
            else:
                raw = [eighth_raw[e][:].rearrange("p j (m t) -> p m j t", t=PACK) for e in range(2)]
                for u in range(2):
                    nc.scalar.copy(dst[u][:, 0:32], raw[0][:, :, :, 2 * u : 2 * u + 2])
                for u in range(2):
                    nc.vector.tensor_copy(out=dst[u][:, 32:64], in_=raw[1][:, :, :, 2 * u : 2 * u + 2])
            for t in (1, 2, 0, 3) if q == 0 else range(PACK):
                cols = slice(t * SLOT + (q + 1) * HALF, t * SLOT + (q + 2) * HALF)
                nc.vector.quantize_mx(
                    out=early_w_codes[:, cols].bitcast(FP8X4),
                    scales=early_w_scales[:, cols],
                    in_=pairs[t // 2][:, t % 2 * QUARTER : (t % 2 + 1) * QUARTER],
                )

        group_and_quantize_quarter(0, 0)
        warm_bank = ypsum.tile([P, PASS], F32, name="ybank")
        for rep in range(WARM):
            nc.tensor.matmul_mx(
                out=warm_bank[0:32, :],
                lhsT=early_w_codes[:, QUARTER : QUARTER + 32].bitcast(FP8X4),
                lhsT_scale=early_w_scales[:, QUARTER : QUARTER + 32],
                rhs=early_w_codes[:, P : P + PASS].bitcast(FP8X4),
                rhs_scale=early_w_scales[:, P : P + PASS],
                start=True,
                stop=True,
            )
        masked_codes = reuse.tile([P, 4 * N], U32, name="masked_codes", offset=0, align_bytes=256)
        nc.vector.memset(masked_codes[:].bitcast(I32), 0)

        late_raw = reuse.tile([P, PACK, PASS], F32, name="late_raw", offset=45056, align_bytes=256)
        w2_raw = reuse.tile([P, 2, PACK, N], F32, name="w2_raw", offset=53760, align_bytes=256)
        pieces = ((0, QUARTER), (QUARTER, P), (QUARTER + P, P))
        for a, w in pieces:
            nc.sync.dma_start(late_raw[:, :, a : a + w], w1_hbm[:, :, PASS + a : PASS + a + w])
        nc.sync.dma_start(w2_raw[:], w2.rearrange("(g p t) n -> p g t n", g=2, t=PACK))

        x_first = keep.tile([P, FIRST], U32, name="x_first", align_bytes=64)
        nc.vector.tensor_copy(
            x_first[:], word_table[:, 0:FIRST_WINDOW].bitcast(U32).indirect(offsets[:, 0 : FIRST // 16])
        )
        group_and_quantize_quarter(1, 24576)
        x_rest = reuse.tile([P, S - FIRST], U32, name="x_rest", offset=24576, align_bytes=64)
        nc.vector.tensor_copy(x_rest[:], word_table[:].bitcast(U32).indirect(offsets[:, FIRST // 16 : S // 16]))

        def tokens(a):
            codes = x_first[:, a : a + TOK] if a < FIRST else x_rest[:, a - FIRST : a - FIRST + TOK]
            return codes.bitcast(FP8X4), x_planes[:].bitcast(U8)[:, a : a + TOK]

        def hidden_pass(dst, codes, scales, cols, a):
            rhs, rhs_scale = tokens(a)
            nc.tensor.matmul_mx(
                out=dst,
                lhsT=codes[:, cols].bitcast(FP8X4),
                lhsT_scale=scales[:, cols],
                rhs=rhs,
                rhs_scale=rhs_scale,
                start=True,
                stop=True,
            )

        def gelu(dst, bank, first=False):
            nc.scalar.activation(
                dst.rearrange("p (n t) -> p n t", t=PACK),
                bank[:].rearrange("p t n -> p n t"),
                GELU,
                bias=warm_out[:] if first else 0.0,
            )

        early_bf = reuse.tile([P, S * PACK], BF16, name="early_bf", offset=4608, align_bytes=64)
        early_codes = keep.tile([P, S], U32, name="early_codes", align_bytes=64)
        early_scales = reuse.tile([P, S], U8, name="early_scales", offset=31744, align_bytes=64)

        for q in range(2):
            for s in range(2):
                upper, lower = (s * TOK, QUARTER + s * TOK) if q == 0 else (QUARTER + s * TOK, s * TOK)
                bank = hpsum.tile([P, PACK, TOK], F32, name="hbank")
                order = range(PACK) if s == 0 else range(PACK - 1, -1, -1)
                for t in order:
                    a = t * SLOT + q * HALF
                    hidden_pass(bank[:, t, :], early_w_codes, early_w_scales, slice(a, a + P), lower)
                    hidden_pass(bank[0:HALF, t, :], early_w_codes, early_w_scales, slice(a + HALF, a + P), upper)
                at = (q * QUARTER + s * TOK) * PACK
                gelu(early_bf[:, at : at + TOK * PACK], bank, first=(q, s) == (0, 0))
        for a in range(FIRST, S, TOK):
            bank = hpsum.tile([P, PACK, TOK], F32, name="hbank")
            for t in range(PACK):
                c0 = t * SLOT + HALF
                hidden_pass(bank[:, t, :], early_w_codes, early_w_scales, slice(c0, c0 + P), a)
            gelu(early_bf[:, a * PACK : (a + TOK) * PACK], bank)

        late_w_codes = keep.tile([P, PASS], U32, name="late_w_codes", align_bytes=64)
        late_w_scales = keep.tile([P, PASS], U8, name="late_w_scales", align_bytes=64)
        for q in range(2):
            grouped = reuse.tile(
                [P, QUARTER * PACK], BF16, name="late_grouped%d" % q, offset=28672 + q * 2048, align_bytes=64
            )
            for a, w in pieces[:1] if q == 0 else pieces[1:]:
                raw = late_raw[:, :, a : a + w].rearrange("p j (m t) -> p m j t", t=PACK)
                rows = slice(a % QUARTER // PACK, (a % QUARTER + w) // PACK)
                for u in range(2):
                    nc.vector.tensor_copy(
                        out=grouped[:].rearrange("p (t m j) -> p m j t", t=PACK, j=PACK)[:, rows, :, 2 * u : 2 * u + 2],
                        in_=raw[:, :, :, 2 * u : 2 * u + 2],
                    )
            for t in range(PACK):
                cols = slice(t * P + q * HALF, t * P + (q + 1) * HALF)
                nc.vector.quantize_mx(
                    out=late_w_codes[:, cols].bitcast(FP8X4),
                    scales=late_w_scales[:, cols],
                    in_=grouped[:, t * QUARTER : (t + 1) * QUARTER],
                )

        w2_codes = keep.tile([P, 2 * N], U32, name="w2_codes", align_bytes=256)
        w2_grouped = reuse.tile([P, 2 * N * PACK], BF16, name="w2_grouped", offset=29696, align_bytes=64)
        for g in range(2):
            nc.vector.tensor_copy(
                out=w2_grouped[:, g * PASS : (g + 1) * PASS].rearrange("p (c i t) -> p c t i", i=4, t=PACK),
                in_=w2_raw[:, g, :, :].rearrange("p t (c i) -> p c t i", i=4),
            )
        for g in range(2):
            nc.vector.quantize_mx(
                out=w2_codes[:, g * N : (g + 1) * N].bitcast(FP8X4),
                scales=w2_scales[:, g * N : (g + 1) * N],
                in_=w2_grouped[:, g * PASS : (g + 1) * PASS],
            )

        def quantize_early(half):
            cols = slice(half * S // 2, (half + 1) * S // 2)
            nc.vector.quantize_mx(
                out=early_codes[:, cols].bitcast(FP8X4),
                scales=early_scales[:, cols],
                in_=early_bf[:, half * S // 2 * PACK : (half + 1) * S // 2 * PACK],
            )

        quantize_early(1)

        top, bottom = slice(0, HALF), slice(HALF, P)
        swapped_scales = keep.tile([P, N], U8, name="swapped_scales", align_bytes=256)
        for i, (dst, src) in enumerate(((top, top), (bottom, bottom), (bottom, top), (top, bottom))):
            move = nc.vector.tensor_copy if i < 2 else nc.sync.dma_start
            move(masked_codes[:].bitcast(I32)[dst, i * N : (i + 1) * N], w2_codes[:].bitcast(I32)[src, 0:N])
        for dst, src in ((bottom, top), (top, bottom)):
            nc.sync.dma_start(swapped_scales[:].bitcast(I32)[dst, :], w2_scales[:].bitcast(I32)[src, 0 : N // 4])

        late_bf = [keep.tile([P, w * PACK], BF16, name="h_bf%d" % c, tag="late%d" % c, align_bytes=256) for c, (a, w) in enumerate(CHUNKS)]
        late_codes = [keep.tile([P, w], U32, name="h_codes%d" % c, align_bytes=64) for c, (a, w) in enumerate(CHUNKS)]
        late_scales = [keep.tile([P, w], U8, name="h_scales%d" % c, align_bytes=64) for c, (a, w) in enumerate(CHUNKS)]

        def late_hidden(c):
            a, w = CHUNKS[c]
            for s in range(w // TOK):
                bank = hpsum.tile([P, PACK, TOK], F32, name="hbank")
                for t in range(PACK) if (c, s) == (0, 0) else reversed(range(PACK)):
                    hidden_pass(bank[:, t, :], late_w_codes, late_w_scales, slice(t * P, (t + 1) * P), a + s * TOK)
                gelu(late_bf[c][:, s * TOK * PACK : (s + 1) * TOK * PACK], bank)
            nc.vector.quantize_mx(out=late_codes[c][:].bitcast(FP8X4), scales=late_scales[c][:], in_=late_bf[c][:])

        def layer2(c):
            a, w = CHUNKS[c]
            acc = ypsum.tile([P, w], F32, name="ybank")
            late = [(w2_codes[:, N : 2 * N], w2_scales[:, N : 2 * N], late_codes[c][:], late_scales[c][:])]
            if a >= FIRST:
                early = [(w2_codes[:, 0:N], w2_scales[:, 0:N], early_codes[:, a : a + w], early_scales[:, a : a + w])]
            else:
                side, b = divmod(a, QUARTER)
                plane = w2_scales[:, 0:N] if side == 0 else swapped_scales[:]
                early = [
                    (
                        masked_codes[:, (2 * side + q) * N : (2 * side + q + 1) * N],
                        plane,
                        early_codes[:, q * QUARTER + b : q * QUARTER + b + w],
                        early_scales[:, q * QUARTER + b : q * QUARTER + b + w],
                    )
                    for q in range(2)
                ]
            passes = early + late if a < FIRST else late + early
            for i, (codes, scales, rhs, rhs_scale) in enumerate(passes):
                nc.tensor.matmul_mx(
                    out=acc[:],
                    lhsT=codes.bitcast(FP8X4),
                    lhsT_scale=scales,
                    rhs=rhs.bitcast(FP8X4),
                    rhs_scale=rhs_scale,
                    start=(i == 0),
                    stop=(i == len(passes) - 1),
                )
            if c >= len(CHUNKS) - 3:
                y = keep.tile([P, w], F32, name="y%d" % c, align_bytes=256)
                nc.scalar.copy(y[:], acc[:])
            else:
                y = keep.tile([P, w], F32, name="y%d" % c, tag="late%d" % (1 - c), align_bytes=256)
                nc.vector.tensor_copy(y[:], acc[:])
            nc.sync.dma_start(out[:, a : a + w], y[:])

        for c in range(len(CHUNKS)):
            late_hidden(c)
            if c == 0:
                quantize_early(0)
            if c >= 1:
                layer2(c - 1)
        layer2(len(CHUNKS) - 1)
